import numpy as np, ml_dtypes
CORES = [16,18,20,22]
N = 4
BF = ml_dtypes.bfloat16
def gentries(a):
    return np.ascontiguousarray(a.reshape(8, 16, -1).transpose(0, 2, 1)).reshape(8, -1)
def gtable(e):
    e = np.asarray(e); return np.ascontiguousarray(e.reshape(8, -1, 16).transpose(0, 2, 1)).reshape(128, -1).astype(np.int32)
S, Q, STEPS = 3072, 128, 2
def whole(rng, *shape):
    return rng.integers(-7, 8, shape).astype(np.float32).astype(BF)
def neighbours(rng, nb):
    own = np.arange(S); nb = np.where(rng.random((N, 8, 1, S)) < 0.0625, own, nb); nb[:, :, 0] = own
    return nb.reshape(N, 128, S).astype(np.int32)
def lists(e):
    return np.stack([gtable(x) for x in e])
def setup_inputs(rng):
    return {"k": whole(rng, N, 128, S), "v": whole(rng, N, 128, S), "nb": neighbours(rng, rng.integers(0, S, (N, 8, 16, S))), "br": rng.integers(0, S, (N, 8, S)).astype(np.int32),
            "q": whole(rng, N, 128, Q), "entry": lists(rng.integers(0, S, (N, 8, Q)))}
def setup_inputs_ties(rng):
    d = setup_inputs(rng); q = np.zeros((N, 8, 16, Q), np.float32)
    for i in range(2): np.put_along_axis(q, rng.integers(0, 16, (N, 8, 1, Q)), rng.choice(np.array([-1, 1], np.float32), (N, 8, 1, Q)), 2)
    q[:, :, :, 3] = 0; d["q"] = q.reshape(N, 128, Q).astype(BF)
    nb = d["nb"].reshape(N, 8, 16, S).copy(); nb[:, :, 9:] = np.where(rng.random((N, 8, 1, S)) < 0.25, nb[:, :, 1:8], nb[:, :, 9:])
    d["nb"] = nb.reshape(N, 128, S); return d
def setup_inputs_ends(rng):
    d = setup_inputs(rng); z = np.array([0, 1, S - 2, S - 1])
    nb = d["nb"].reshape(N, 8, 16, S); nb = np.where(rng.random(nb.shape) < 0.5, z[rng.integers(0, 4, nb.shape)], nb); nb[:, :, 0] = np.arange(S); nb[:, :, :, S - 2] = S - 2
    br = d["br"]; d["br"] = np.where(rng.random(br.shape) < 0.5, z[rng.integers(0, 4, br.shape)], br).astype(np.int32)
    e = z[rng.integers(0, 4, (N, 8, Q))]; e[:, :, 0] = S - 1; e[:, :, 1] = S - 2; d["entry"] = lists(e)
    q = d["q"].astype(np.float32).reshape(N, 8, 16, Q); q[:, :, :, :2] = 7 * rng.choice(np.array([-1, 1], np.float32), (N, 8, 16, 2))
    k = d["k"].astype(np.float32).reshape(N, 8, 16, S); k[:, :, :, S - 1] = q[:, :, :, 0]; k[:, :, :, S - 2] = -q[:, :, :, 1]
    d["nb"] = nb.reshape(N, 128, S).astype(np.int32); d["q"] = q.reshape(N, 128, Q).astype(BF); d["k"] = k.reshape(N, 128, S).astype(BF); return d
def setup_inputs_one(rng):
    d = setup_inputs(rng); e = rng.integers(0, S, (N, 8, 1)); b = rng.integers(0, S, (N, 8, 1))
    d["entry"] = lists(np.repeat(e, Q, axis=2)); d["br"] = np.repeat(b, S, axis=2).astype(np.int32); return d
def setup_inputs_spread(rng):
    d = setup_inputs(rng)
    for a in ("k", "v", "q"):
        z = rng.choice(np.array([0, 1, 2, 3, 5, 7, 7, 7]), (N, 8, 1, d[a].shape[-1])); d[a] = rng.integers(-z, z + 1, (N, 8, 16, d[a].shape[-1])).reshape(d[a].shape).astype(np.float32).astype(BF)
    low = lambda *shape: np.minimum(np.floor(S * rng.random(shape) ** 4), S - 1).astype(np.int64)
    nb = neighbours(rng, low(N, 8, 16, S)).reshape(N, 8, 16, S); nb[:, :, 2:] = np.where(rng.random((N, 8, 1, S)) < 0.25, nb[:, :, 1:2], nb[:, :, 2:])
    d["nb"] = nb.reshape(N, 128, S); d["br"] = low(N, 8, S).astype(np.int32); d["entry"] = lists(low(N, 8, Q)); return d
def check_inputs(d):
    bad = []
    for a in ("k", "v", "q"):
        x = d[a].astype(np.float32)
        if not ((np.abs(x) <= 7) & (np.rint(x) == x)).all(): bad.append(a + "_whole")
    for a in ("nb", "br", "entry"):
        if not ((d[a] >= 0) & (d[a] < S)).all(): bad.append(a + "_range")
    if not (d["nb"][:, ::16] == np.arange(S)).all(): bad.append("nb_self")
    return bad
def reference(k, v, nb, br, q, entry):
    y = np.zeros((N, 8, 16, Q), np.int64); gr = np.arange(8)[:, None, None, None]; ft = np.arange(16)[None, :, None, None]
    keys = k.astype(np.float32).astype(np.int32).reshape(N, 8, 16, S); vals = v.astype(np.float32).astype(np.int32).reshape(N, 8, 16, S)
    nbs = nb.reshape(N, 8, 16, S); qs = q.astype(np.float32).astype(np.int32).reshape(N, 8, 16, Q)
    for r in range(N):
        at = gentries(entry[r])
        for s in range(N):
            t = (r + s) % N
            for step in range(STEPS):
                c = np.take_along_axis(nbs[t], at[:, None], 2)
                score = np.sum(keys[t][gr, ft, c[:, None]] * qs[r][:, :, None], axis=1)
                p = np.argmax(score, axis=1)[:, None]
                at = np.take_along_axis(c, p, 1)[:, 0]; best = np.take_along_axis(score, p, 1)
            y[r] += np.maximum(best, 0) * np.take_along_axis(vals[t], at[:, None], 2)
            at = np.take_along_axis(br[t], at, 1)
    return {"y": y.reshape(N, 128, Q).astype(np.float32)}

@@ -1,0 +1,290 @@
+from concourse.bass import DstId, RemoteDMATransfer
+from concourse.mybir import AluOpType, ActivationFunctionType
+
+S, Q, N = 3072, 128, 4
+HALF = S // 2
+SUBS = [(0, 4), (4, 4)]
+MAXS = 4
+KA = 1024
+ENG = "VSS"
+NB2 = "SVSVSVSV"
+PIECES = [[30, 12, 22], [16, 28, 20], [24, 28, 12], [16, 26, 22], [32, 16, 16], [36, 22, 6], [12, 24, 28], [30, 14, 20], [12, 28, 24], [12, 32, 20], [20, 32, 12], [32, 4, 28], [14, 28, 22], [6, 56, 2], [24, 8, 32], [10, 22, 32]]
+FLIP = [50, 51, 52, 53, 54, 55, 56, 96, 134, 153, 157, 159, 169, 174, 183, 193, 195, 199, 215, 219, 221, 237, 255, 257, 261, 268, 271, 275, 277, 287, 290, 293, 295, 309, 311, 313, 315, 330, 333, 335, 339, 353, 355, 385, 389, 391, 399]
+ORDER = [0,1,2,3,4,8,5,11,7,6,9,10,12,16,15,14,17,21,19,37,41,35,23,30,18,32,93,94,36,38,22,31,33,26,25,39,24,27,28,40,44,42,45,43,46,34,65,57,66,58,60,62,61,29,64,63,59,95,133,20,47,91,13,134,96,48,55,51,53,99,75,137,54,50,52,103,101,135,97,98,104,100,102,105,68,83,72,88,106,107,85,108,76,109,74,110,139,141,140,136,142,138,111,143,115,144,145,146,112,147,148,149,78,157,49,117,119,113,118,116,120,121,73,150,79,153,155,114,154,122,158,151,123,82,124,125,81,126,77,89,67,70,86,129,69,156,159,152,160,161,162,163,164,90,84,71,80,130,131,56,92,87,167,132,127,128,173,174,175,181,182,177,178,179,180,176,165,166,211,215,183,184,168,212,219,185,186,169,187,188,189,213,216,220,217,218,214,221,193,197,195,222,223,224,190,225,226,227,196,191,194,198,192,233,228,199,234,200,229,231,235,232,236,230,201,202,203,204,237,238,207,208,239,240,241,242,209,170,245,210,205,206,251,252,255,257,243,244,253,256,259,258,260,254,289,297,261,262,298,246,295,296,263,264,265,266,267,293,294,299,275,290,247,291,292,300,301,302,303,304,248,305,268,273,313,271,276,269,274,272,270,277,278,279,306,280,311,281,314,307,309,312,310,282,171,172,249,283,315,285,308,286,316,317,318,319,320,321,323,324,284,325,329,287,337,333,335,330,322,365,369,338,336,334,331,339,332,340,341,342,366,343,344,345,288,373,371,370,374,372,346,375,349,326,367,368,376,377,378,379,380,353,351,350,347,381,250,382,387,348,354,352,355,385,389,383,388,356,390,386,327,328,357,358,391,359,384,392,360,361,393,362,363,394,395,396,397,364,398,399,400,401,404,402,405,403,406]
+
+SCRATCH = {
+    "nbw": ("sbuf", [128, S], "int32"), "kw": ("sbuf", [128, S], "bfloat16"), "vw": ("sbuf", [128, S], "bfloat16"),
+    "nb2": ("sbuf", [128, S], "float32"), "blo": ("sbuf", [128, 192], "uint16"), "bli": ("sbuf", [128, 192], "uint16"),
+    "brs": ("sbuf", [128, 768], "int32"), "brh": ("sbuf", [128, 768], "float16"),
+    "qall": ("sbuf", [128, N * Q], "bfloat16"), "qblk": ("sbuf", [128, 8 * N * Q], "bfloat16"),
+    "ent": ("sbuf", [128, 8], "int32"),
+    "lst": ("sbuf", [128, 8 * 16 * MAXS], "uint16"), "lin": ("sbuf", [128, 8 * 3 * MAXS], "uint16"),
+    "cu": ("sbuf", [128, 64 * MAXS], "uint16"), "ch": ("sbuf", [128, 80 * MAXS], "float16"),
+    "kg": ("sbuf", [128, 1024 * MAXS], "bfloat16"), "bsb": ("sbuf", [128, 128 * MAXS], "float16"),
+    "rr": ("sbuf", [128, 68 * MAXS], "float32"), "nf": ("sbuf", [128, 68 * MAXS], "float32"), "yy": ("sbuf", [128, 68 * MAXS], "float32"),
+    "kq": ("sbuf", [128, N * Q], "bfloat16"), "rs": ("sbuf", [128, N * Q], "float32"),
+    "term": ("sbuf", [128, N * Q], "float32"), "acc": ("sbuf", [128, N * Q], "float32"),
+    "pi": ("sbuf", [128, 4], "int32"), "pb": ("sbuf", [128, 4], "int32"), "pf": ("sbuf", [128, 4], "float32"),
+    "i8": ("sbuf", [128, 8], "float32"), "ig": ("sbuf", [128, 128], "float32"),
+    "i17": ("sbuf", [128, 68], "float32"), "iz": ("sbuf", [128, 68], "float32"), "iu": ("sbuf", [128, 36], "float32"),
+    "ie": ("sbuf", [128, 576], "float32"), "m4": ("sbuf", [128, 4], "float32"), "hb": ("sbuf", [128, 4], "float32"),
+    "gm8": ("sbuf", [128, 8], "float32"), "bones": ("sbuf", [128, 128], "bfloat16"),
+    "reset": ("sbuf", [128, 68], "float32"), "sel": ("sbuf", [128, 68], "float16"),
+    "t1": ("sbuf", [128, 68], "float32"), "t2": ("sbuf", [128, 68], "float32"), "t3": ("sbuf", [128, 68], "float32"),
+    "t4": ("sbuf", [128, 68], "float32"), "t5": ("sbuf", [128, 68], "float32"), "m16": ("sbuf", [128, 4], "float32"),
+    "a1": ("sbuf", [128, 36], "float32"), "a2": ("sbuf", [128, 36], "float32"), "a3": ("sbuf", [128, 36], "float32"),
+    "dif": ("sbuf", [128, 36], "float16"), "e4": ("sbuf", [128, 576], "float16"),
+}
+for _b in range(8):
+    SCRATCH["ps%d" % _b] = ("psum", [128, 512], "float32")
+SEMAPHORES = (["cV", "cS", "cP", "cG", "ldq", "ldb", "lde", "ldn", "ldk", "ldk2", "ldv", "sent", "qarr", "bla"]
+              + ["la%d_%d" % (s, h) for s in range(3) for h in range(MAXS)]
+              + ["aa%d" % s for s in range(3)] + ["fa%d" % h for h in range(MAXS)] + ["st%d" % h for h in range(MAXS)])
+
+
+def build(g, core, T, topo):
+    A, F = AluOpType, ActivationFunctionType
+    NS = len(SUBS)
+    rank = T.rank_of(core)
+    nxt, prv = T.cores[(rank + 1) % N], T.cores[(rank - 1) % N]
+    rid, pid, _se = topo.addr(nxt)
+    mask = topo.mask(core, nxt)
+    n_out, n_in = len(topo.engines(core, nxt)), len(topo.engines(prv, core))
+    V, Sc, P, Y = g.vector, g.scalar, g.tensor, g.sync
+    ops, banks, sent, lead = [], {}, [0], [0]
+
+    def op(q, kind, n, needs, emit, sig=None, bank=None, tag=None, alt=None):
+        needs = [x for x in needs if x is not None]
+        if bank is not None:
+            st = banks.setdefault(bank, [q, [], []])
+            if st[0] != q:
+                st[0], st[2], st[1] = q, st[1], []
+            needs = needs + st[2]
+            st[1].append(len(ops))
+        ops.append([q, kind, n, sorted(set(needs)), emit, sig, lead[0], tag, alt])
+        return len(ops) - 1
+
+    def either(e, fv, fs, needs, bank=None, tag=None):
+        if len(ops) in FLIP: e = "S" if e == "V" else "V"
+        a, b = (fv, fs) if e == "V" else (fs, fv)
+        return op(e, a[0], a[1], needs, a[2], bank=bank, tag=tag, alt=("S" if e == "V" else "V", b[0], b[1]))
+    def copy(e, out, a, needs, n, kind="c", bank=None, tag=None):
+        return either(e, (kind, n, lambda: V.tensor_copy(out, a)), (kind, n, lambda: Sc.activation(out, a, F.Copy)), needs, bank, tag)
+    def ts(out, in0, s1, s2, o0, o1, needs, n, bank=None):
+        if o1 is None: return op("V", "c", n, needs, lambda: V.tensor_scalar(out, in0, s1, None, o0), bank=bank)
+        return op("V", "c", n, needs, lambda: V.tensor_scalar(out, in0, s1, s2, o0, o1), bank=bank)
+    def tt(out, a, b, o, needs, n, kind="c", bank=None):
+        return op("V", kind, n, needs, lambda: V.tensor_tensor(out, a, b, o), bank=bank)
+    def cp(out, a, needs, n, kind="c"):
+        return op("V", kind, n, needs, lambda: V.tensor_copy(out, a))
+    def scan(out, d0, d1, o0, o1, needs, n, bank=None):
+        return op("V", "c", n, needs, lambda: V.tensor_tensor_scan(out, d0, d1, 0.0, o0, o1), bank=bank)
+    def mm(lst, needs, bank, tag=None, add=False):
+        def emit():
+            for x, (o, l, r) in enumerate(lst): ins = P.matmul(o, l, r, x == 0 or not add, x == len(lst) - 1 or not add)
+            return ins
+        return op("P", "p", sum(max(min(64, l.shape[-1]), r.shape[-1]) for (o, l, r) in lst), needs, emit, bank=bank, tag=tag)
+    def iota(out, pat, cm, n, base=0):
+        return op("G", "i", n, [], lambda: g.iota(out, pat, base, cm, allow_small_or_imprecise_dtypes=True))
+    def dma(q, out, in_, sem, n, needs=()):
+        e = Y if q == "Y" else Sc
+        return op(q, "d", n, list(needs), lambda: e.dma_start(out, in_), sig=(sem, 16))
+    def send(emit, needs, sem, cnt, n_loc, n, after=()):
+        sent[0] += n_loc
+        a = op("G", "r", 2000 if sem == "qarr" else 0, needs, emit, sig=("sent", None))
+        return op(None, "a", n, [a] + list(after), None, sig=(sem, cnt))
+
+    qs = lambda r, a=0, b=Q: T.qall[:, r * Q + a:r * Q + b]
+    lead[0] = -1
+    ldq = dma("Y", qs(rank), T.q[:], "ldq", 4e4)
+    ldb = dma("S", T.brs[0:32, :], T.br[:], "ldb", 14e4)
+    lde = dma("S", T.ent[:], T.entry[:], "lde", 16e4)
+    lead[0] = 0
+    ldn = dma("Y", T.nbw[:], T.nb[:], "ldn", 176e4)
+    ldk = dma("S", T.kw[:, 0:KA], T.k[:, 0:KA], "ldk", 256e4)
+
+    others = [c for c in T.cores if c != core]
+    def qmask(c):
+        m = -1
+        for d in T.cores:
+            if d != c: m &= topo.mask(c, d)
+        return m
+    bits = lambda m: bin(m).count("1")
+    def qsend():
+        ids = [DstId(rid=topo.addr(d)[0], pnc=topo.addr(d)[1]) for d in others]
+        tr = RemoteDMATransfer(dst_ids=ids, dma_engine_mask=qmask(core), remote_sem=T.sem.qarr, srcs=[qs(rank)], dsts=[qs(rank)] * len(others))
+        return g.remote_dma_fused([tr], local_sem=T.sem.sent)
+
+    gp = op("G", "i", 1, [], lambda: g.iota(T.pi[:, 0:1], [[0, 1]], 0, 1))
+    g8 = iota(T.i8[:], [[1, 8]], 0, 8)
+    ge = iota(T.ie[0:32, :], [[4, 4], [1, 144]], -4, 576, -15)
+    g17 = iota(T.i17[:], [[0, 4], [1, 17]], 0, 68)
+    gz = iota(T.iz[:], [[32, 4], [1, 17]], -1, 68)
+    gu = iota(T.iu[:, 0:34], [[16, 2], [1, 17]], 0, 34)
+    gg = iota(T.ig[:], [[1, 8], [0, 16]], 0, 128)
+    qarr = send(qsend, [ldq, gp, g8, ge, g17, gz, gu, gg], "qarr", sum(bits(qmask(c)) for c in others), bits(qmask(core)), 0, [ldn])
+    b0 = ts(T.pb[:, 0:1], T.pi[:, 0:1], 3, None, A.bitwise_and, None, [gp], 1)
+    b1 = ts(T.pb[:, 1:2], T.pi[:, 0:1], 31, None, A.bitwise_and, None, [gp], 1)
+    b2 = ts(T.pb[:, 2:3], T.pi[:, 0:1], 4, None, A.arith_shift_right, None, [gp], 1)
+    pf = cp(T.pf[:, 0:3], T.pb[:, 0:3], [b0, b1, b2], 3)
+    p3, p31, pg = T.pf[:, 0:1], T.pf[:, 1:2], T.pf[:, 2:3]
+    hb = op("V", "c", 1, [], lambda: V.memset(T.hb[:], -float(HALF)))
+    gm8 = ts(T.gm8[:], T.i8[:], pg, None, A.is_equal, None, [pf, g8], 8)
+    bones = ts(T.bones[:], T.ig[:], pg, None, A.is_equal, None, [pf, gg], 128)
+    m4 = ts(T.m4[:], T.i8[:, 0:4], p3, None, A.is_equal, None, [pf, g8], 4)
+    reset = ts(T.reset[:], T.i17[:], 0.0, -1000000.0, A.is_equal, A.mult, [g17], 68)
+    m16 = ts(T.m16[:, 0:1], T.pi[:, 0:1], 16.0, None, A.is_equal, None, [gp], 1)
+    t1 = ts(T.t1[:], T.iz[:], 0.0, 16.0, A.is_equal, A.mult, [gz], 68)
+    t2 = ts(T.t2[:], T.i17[:], 16.0, -30000.0, A.is_equal, A.mult, [g17], 68)
+    t3 = ts(T.t3[:], T.i17[:], -1.0, 15.0, A.mult, A.add, [g17], 68)
+    t4 = tt(T.t4[:], T.t3[:], T.t2[:], A.add, [t2, t3], 136)
+    t5 = ts(T.t5[:], T.t4[:], T.m16[:, 0:1], None, A.mult, None, [t4, m16], 68)
+    sel = tt(T.sel[:], T.t5[:], T.t1[:], A.add, [t5, t1], 136)
+    a1 = ts(T.a1[:, 0:34], T.iu[:, 0:34], -1.0, p31, A.add, A.is_equal, [gu, pf], 34)
+    a2 = ts(T.a2[:, 0:34], T.iu[:, 0:34], p31, None, A.is_equal, None, [gu, pf], 34)
+    a3 = ts(T.a3[:, 0:34], T.i17[:, 0:34], 16.0, None, A.not_equal, None, [g17], 34)
+    a4 = tt(T.a2[:, 0:34], T.a2[:, 0:34], T.a3[:, 0:34], A.mult, [a2, a3], 68)
+    dif = tt(T.dif[:, 0:34], T.a1[:, 0:34], T.a2[:, 0:34], A.subtract, [a1, a4], 68)
+    e4 = [ts(T.e4[0:32, 144 * x:144 * x + 144], T.ie[0:32, 144 * x:144 * x + 144], 0.0, T.m4[0:32, x:x + 1], A.is_equal, A.mult, [ge, m4], 144) for x in range(4)]
+    pad = [ts(T.ch[:, 80 * h:80 * h + 16], T.i17[:, 0:16], 0.0, None, A.mult, None, [g17], 16) for h in range(NS)]
+    PA = [T["ps%d" % h] for h in range(NS)]
+    PK = [T["ps%d" % (NS + h)] for h in range(NS)]
+    own_s = 3 * NS <= 6
+    bS = [2 * NS + h if own_s else h for h in range(NS)]
+    cS = 0 if own_s else 128
+
+    brh = ts(T.brh[0:32, :], T.brs[0:32, :], -float(HALF), None, A.add, None, [ldb], 768)
+    bl = [mm([(T.ps7[:, 48 * x:48 * x + 48], T.e4[0:32, 144 * x + 15 - b:144 * x + 143 - b], T.brh[0:32, b::16]) for b in range(16)],
+             [brh, e4[x]], 7, add=True) for x in range(4)]
+    blo = ts(T.blo[:], T.ps7[:, 0:192], float(HALF), None, A.add, None, bl, 192, bank=7)
+    bla = send(lambda: g.remote_dma(T.bli[:], T.blo[:], T.sem.bla, T.sem.sent, pid, rid, mask), [blo, qarr - 1], "bla", n_in, n_out, 0, [ldn])
+    z = 192 // len(NB2)
+    nb2 = [copy(e, T.nb2[:, 16 * z * x:16 * z * (x + 1)], T.nbw[:, :].indirect(T.bli[:, z * x:z * (x + 1)]), [bla, ldn], 16 * z, "g", tag="b")
+           for x, e in enumerate(NB2)]
+    ones = [op("V", "c", 128, [blo], (lambda h=h: V.memset(PA[h][:, 0:128], 1.0)), bank=h) for h in range(NS)]
+
+    qb = {}
+    for s in range(N):
+        r = (rank - s) % N
+        qb[s] = [ts(T.qblk[:, x * N * Q + r * Q:x * N * Q + r * Q + Q], qs(r), T.gm8[:, x:x + 1], None, A.mult, None,
+                    [gm8] + ([ldq, blo] if s == 0 else [qarr]), 64) for x in range(8)]
+
+    ldk2 = dma("Y", T.kw[:, KA:S], T.k[:, KA:S], "ldk2", 52e4, qb[0] + ones)
+    ldv = dma("Y", T.vw[:], T.v[:], "ldv", 79e4, [ldn, ldk, ldk2])
+    slot = [0]
+    def newlist(w):
+        slot[0] += 1
+        return T.lst[:, 8 * (slot[0] - 1):8 * (slot[0] - 1) + w]
+
+    cur = []
+    for h, (a0, w) in enumerate(SUBS):
+        L = newlist(w)
+        cur.append((L, cp(L, T.ent[:, a0:a0 + w], [lde], 8)))
+    last = [None] * NS
+    accin = None
+    for s in range(N):
+        r = (rank - s) % N
+        terms = []
+        for h, (a0, w) in enumerate(SUBS):
+            n, m = 16 * w, 17 * w
+            L, rdy = cur[h]
+            lead[0] = NS - h
+            cu, ch, kg = T.cu, T.ch, T.kg
+            c0, h0, k0 = 64 * h, 80 * h, 1024 * h
+            rr, nf, yy = (x[:, 68 * h:68 * h + m] for x in (T.rr, T.nf, T.yy))
+            K, E = PK[h][:, 0:m], PK[h][:, 128:128 + m]
+            for step in range(2):
+                far = s > 0 and step == 0
+                win = (T.nb2 if far else T.nbw)[:, :].indirect(L)
+                cc, cf = cu[:, c0:c0 + n], ch[:, h0 + 16:h0 + 16 + n]
+                cg = cp(cc, win, [rdy, last[h]] + (nb2 if far else [ldn]), n, "g")
+                c16 = either("V", ("c", n // 2, lambda cf=cf, cc=cc: V.tensor_scalar(cf, cc, -float(HALF), None, A.add)),
+                             ("g", n, lambda cf=cf, win=win: Sc.activation(cf, win, F.Identity, bias=T.hb[:, 0:1])), [cg, pad[h], hb])
+                m1 = mm([(PK[h][32 * G:32 * G + 32, 128 + 17 * a:128 + 17 * a + 17], ch[32 * G:32 * G + 32, h0 + 16 * a:h0 + 16 * a + 32],
+                          T.dif[32 * G:32 * G + 32, 17:34]) for G in range(4) for a in range(w)], [c16, dif], NS + h)
+                m0 = mm([(PK[h][32 * G:32 * G + 16, 128 + 17 * a:128 + 17 * a + 17], ch[32 * G:32 * G + 32, h0 + 16 * a + 16:h0 + 16 * a + 32],
+                          T.dif[32 * G:32 * G + 32, 0:17]) for G in range(4) for a in range(w)], [m1], NS + h)
+                pe1, j0 = [], 0
+                for x, (e, cnt) in enumerate(zip(ENG, PIECES[(s * NS + h) * 2 + step])):
+                    tag = ((s * NS + h) * 2 + step, x)
+                    ga = copy(e, kg[:, k0 + 16 * j0:k0 + 16 * (j0 + cnt)], T.kw[:, :].indirect(cu[:, c0 + j0:c0 + j0 + cnt]), [cg, ldk, ldk2], 16 * cnt, "g", tag=tag)
+                    pe1.append(mm([(PA[h][32 * (j // 16):32 * (j // 16) + 16, (j % 16):128:16], kg[:, k0 + 16 * j:k0 + 16 * j + 16],
+                                    T.qblk[:, r * Q + 16 * a0 + j::N * Q]) for j in range(j0, j0 + cnt)], [ga] + qb[s] + [ones[h]], h, tag))
+                    j0 += cnt
+                B = T.bsb[0:32 * w, 128 * h:128 * h + 128]
+                ev = copy("V", B, PA[h][0:32 * w, 0:128], pe1, 128, bank=h)
+                p2 = mm([(K, B, T.sel[0:32 * w, 0:m])], [ev, sel], NS + h)
+                s1 = scan(rr, T.reset[:, 0:m], K, A.add, A.max, [p2, reset], m, bank=NS + h)
+                lt = tt(nf, K, rr, A.is_lt, [s1], m, bank=NS + h)
+                s2 = scan(yy, E, nf, A.add, A.mult, [lt, m0], m, bank=NS + h)
+                L = newlist(w)
+                rdy = ts(L, T.yy[:, 68 * h + 16:68 * h + m:17], float(HALF), None, A.add, None, [s2], w)
+                last[h] = rdy
+            x0 = s * Q + 16 * a0
+            if s < N - 1:
+                Li = T.lin[:, 8 * (s * NS + h):8 * (s * NS + h) + w]
+                sem = "la%d_%d" % (s, h)
+                cur[h] = (Li, send((lambda Li=Li, L=L, sem=sem: g.remote_dma(Li, L, T.sem[sem], T.sem.sent, pid, rid, mask)), [rdy], sem, n_in, n_out, 0))
+            kq = tt(T.kq[:, x0:x0 + n], T.kw[:, :].indirect(L), qs(r, 16 * a0, 16 * a0 + n), A.mult, [rdy, ldq if s == 0 else qarr], n, "g")
+            ps, rs = T["ps%d" % bS[h]][:, cS:cS + n], T.rs[:, x0:x0 + n]
+            sm = mm([(ps, T.bones[:], T.kq[:, x0:x0 + n])], [kq, bones], bS[h])
+            rl = either("S", ("c", n, lambda rs=rs, ps=ps: V.tensor_scalar(rs, ps, 0.0, None, A.max)),
+                        ("c", n, lambda rs=rs, ps=ps: Sc.activation(rs, ps, F.Relu)), [sm], bank=bS[h])
+            terms.append(tt(T.term[:, x0:x0 + n], T.vw[:, :].indirect(L), rs, A.mult, [rl, ldv], n, "g"))
+
+        def accsend(a, b, sem, s=s):
+            dst, src = T.acc[:, s * Q + a:s * Q + b], T.term[:, s * Q + a:s * Q + b]
+            if s == 0: return g.remote_dma(dst, src, T.sem[sem], T.sem.sent, pid, rid, mask)
+            tr = RemoteDMATransfer(dst_ids=[DstId(rid=rid, pnc=pid)], dma_engine_mask=mask, remote_sem=T.sem[sem],
+                                   srcs=[src, T.acc[:, (s - 1) * Q + a:(s - 1) * Q + b]], dsts=[dst], alu_op=1)
+            return g.remote_dma_fused([tr], local_sem=T.sem.sent)
+        if s < N - 1:
+            accin = send((lambda f=accsend, s=s: f(0, Q, "aa%d" % s)), terms + [accin], "aa%d" % s, n_in, n_out, 13e4)
+        else:
+            for h, (a0, w) in enumerate(SUBS):
+                a, b = 16 * a0, 16 * (a0 + w)
+                fa = send((lambda f=accsend, a=a, b=b, h=h: f(a, b, "fa%d" % h)), [terms[h], accin], "fa%d" % h, n_in, n_out, 16384 * w)
+                dma("Y", T.y[:, a:b], T.acc[:, s * Q + a:s * Q + b], "st%d" % h, 8192 * w, [fa])
+    return ops, sent[0]
+
+
+def rank_program(g, core, T, topo):
+    if T.rank_of(core) is None:
+        return
+    ops, sent = build(g, core, T, topo)
+    pos = {i: x for x, i in enumerate(ORDER)}
+    queue = {"V": g.vector, "S": g.scalar, "P": g.tensor, "G": g, "Y": g.sync}
+    count = {"cV": 0, "cS": 0, "cP": 0, "cG": 0}
+    known = {q: {} for q in queue}
+    sig, clock, stores = {}, {}, []
+    for i in ORDER:
+        q, needs, emit, sg = ops[i][0], ops[i][3], ops[i][4], ops[i][5]
+        if q is None:
+            sig[i], clock[i] = sg, {sg[0]: sg[1]}
+            continue
+        kn = known[q]
+        for d in sorted(needs, key=lambda d: -pos[d]):
+            sem, cnt = sig[d]
+            if kn.get(sem, 0) >= cnt: continue
+            queue[q].wait_ge(T.sem[sem], cnt)
+            for k2, v2 in clock[d].items():
+                if kn.get(k2, 0) < v2: kn[k2] = v2
+        ins = emit()
+        if sg is None:
+            sem = "c" + q
+            count[sem] += 1
+            ins.then_inc(T.sem[sem], 1)
+            sig[i] = (sem, count[sem])
+        elif sg[1] is None:
+            sig[i] = (sg[0], 0)
+        else:
+            ins.then_inc(T.sem[sg[0]], sg[1])
+            sig[i] = sg
+            if sg[0].startswith("st"): stores.append(sg)
+        clock[i] = dict(kn)
+        clock[i][sig[i][0]] = sig[i][1]
+    for sem in ("cG", "cP", "cS", "cV"):
+        g.wait_ge(T.sem[sem], count[sem])
+    g.wait_ge(T.sem.sent, sent)
+    for sem, cnt in stores:
+        g.sync.wait_ge(T.sem[sem], cnt)

@@ -3,14 +3,13 @@ from concourse.mybir import AluOpType, ActivationFunctionType
 
 S, Q, N = 3072, 128, 4
 HALF = S // 2
-SUBS = [(0, 4), (4, 4)]
-MAXS = 4
+SUBS = [(0, 3), (3, 3), (6, 2)]
+NS, W = len(SUBS), max(w for _a, w in SUBS)
+PIECES = {4: [20, 20, 12, 12], 3: [16, 16, 8, 8], 2: [12, 12, 8]}
 KA = 1024
-ENG = "VSS"
-NB2 = "SVSVSVSV"
-PIECES = [[30, 12, 22], [16, 28, 20], [24, 28, 12], [16, 26, 22], [32, 16, 16], [36, 22, 6], [12, 24, 28], [30, 14, 20], [12, 28, 24], [12, 32, 20], [20, 32, 12], [32, 4, 28], [14, 28, 22], [6, 56, 2], [24, 8, 32], [10, 22, 32]]
-FLIP = [50, 51, 52, 53, 54, 55, 56, 96, 134, 153, 157, 159, 169, 174, 183, 193, 195, 199, 215, 219, 221, 237, 255, 257, 261, 268, 271, 275, 277, 287, 290, 293, 295, 309, 311, 313, 315, 330, 333, 335, 339, 353, 355, 385, 389, 391, 399]
-ORDER = [0,1,2,3,4,8,5,11,7,6,9,10,12,16,15,14,17,21,19,37,41,35,23,30,18,32,93,94,36,38,22,31,33,26,25,39,24,27,28,40,44,42,45,43,46,34,65,57,66,58,60,62,61,29,64,63,59,95,133,20,47,91,13,134,96,48,55,51,53,99,75,137,54,50,52,103,101,135,97,98,104,100,102,105,68,83,72,88,106,107,85,108,76,109,74,110,139,141,140,136,142,138,111,143,115,144,145,146,112,147,148,149,78,157,49,117,119,113,118,116,120,121,73,150,79,153,155,114,154,122,158,151,123,82,124,125,81,126,77,89,67,70,86,129,69,156,159,152,160,161,162,163,164,90,84,71,80,130,131,56,92,87,167,132,127,128,173,174,175,181,182,177,178,179,180,176,165,166,211,215,183,184,168,212,219,185,186,169,187,188,189,213,216,220,217,218,214,221,193,197,195,222,223,224,190,225,226,227,196,191,194,198,192,233,228,199,234,200,229,231,235,232,236,230,201,202,203,204,237,238,207,208,239,240,241,242,209,170,245,210,205,206,251,252,255,257,243,244,253,256,259,258,260,254,289,297,261,262,298,246,295,296,263,264,265,266,267,293,294,299,275,290,247,291,292,300,301,302,303,304,248,305,268,273,313,271,276,269,274,272,270,277,278,279,306,280,311,281,314,307,309,312,310,282,171,172,249,283,315,285,308,286,316,317,318,319,320,321,323,324,284,325,329,287,337,333,335,330,322,365,369,338,336,334,331,339,332,340,341,342,366,343,344,345,288,373,371,370,374,372,346,375,349,326,367,368,376,377,378,379,380,353,351,350,347,381,250,382,387,348,354,352,355,385,389,383,388,356,390,386,327,328,357,358,391,359,384,392,360,361,393,362,363,394,395,396,397,364,398,399,400,401,404,402,405,403,406]
+NB2 = 8
+C_LO, C_HI = 64.0, 4096.0
+COST = dict(cycle=0.00092, gather=1.5, pe=0.00046, wait=0.2, dma=1.0, rate=3e5, issue=0.3, first=2.0, remote=1.2, look=0.5, margin=0.2, spare=0.1, lead=0.6)
 
 SCRATCH = {
     "nbw": ("sbuf", [128, S], "int32"), "kw": ("sbuf", [128, S], "bfloat16"), "vw": ("sbuf", [128, S], "bfloat16"),
@@ -18,90 +17,92 @@ SCRATCH = {
     "brs": ("sbuf", [128, 768], "int32"), "brh": ("sbuf", [128, 768], "float16"),
     "qall": ("sbuf", [128, N * Q], "bfloat16"), "qblk": ("sbuf", [128, 8 * N * Q], "bfloat16"),
     "ent": ("sbuf", [128, 8], "int32"),
-    "lst": ("sbuf", [128, 8 * 16 * MAXS], "uint16"), "lin": ("sbuf", [128, 8 * 3 * MAXS], "uint16"),
-    "cu": ("sbuf", [128, 64 * MAXS], "uint16"), "ch": ("sbuf", [128, 80 * MAXS], "float16"),
-    "kg": ("sbuf", [128, 1024 * MAXS], "bfloat16"), "bsb": ("sbuf", [128, 128 * MAXS], "float16"),
-    "rr": ("sbuf", [128, 68 * MAXS], "float32"), "nf": ("sbuf", [128, 68 * MAXS], "float32"), "yy": ("sbuf", [128, 68 * MAXS], "float32"),
+    "lst": ("sbuf", [128, 8 * 9 * NS], "uint16"), "lin": ("sbuf", [128, 8 * 3 * NS], "uint16"),
+    "cu": ("sbuf", [128, 64 * NS], "uint16"), "ch": ("sbuf", [128, 64 * NS], "float16"),
+    "kg": ("sbuf", [128, 1024 * NS], "bfloat16"), "bs": ("sbuf", [128, 128 * NS], "float16"), "bx": ("sbuf", [128, 128 * NS], "float16"),
+    "rr": ("sbuf", [128, 192 * NS], "float32"),
     "kq": ("sbuf", [128, N * Q], "bfloat16"), "rs": ("sbuf", [128, N * Q], "float32"),
     "term": ("sbuf", [128, N * Q], "float32"), "acc": ("sbuf", [128, N * Q], "float32"),
     "pi": ("sbuf", [128, 4], "int32"), "pb": ("sbuf", [128, 4], "int32"), "pf": ("sbuf", [128, 4], "float32"),
-    "i8": ("sbuf", [128, 8], "float32"), "ig": ("sbuf", [128, 128], "float32"),
-    "i17": ("sbuf", [128, 68], "float32"), "iz": ("sbuf", [128, 68], "float32"), "iu": ("sbuf", [128, 36], "float32"),
-    "ie": ("sbuf", [128, 576], "float32"), "m4": ("sbuf", [128, 4], "float32"), "hb": ("sbuf", [128, 4], "float32"),
-    "gm8": ("sbuf", [128, 8], "float32"), "bones": ("sbuf", [128, 128], "bfloat16"),
-    "reset": ("sbuf", [128, 68], "float32"), "sel": ("sbuf", [128, 68], "float16"),
-    "t1": ("sbuf", [128, 68], "float32"), "t2": ("sbuf", [128, 68], "float32"), "t3": ("sbuf", [128, 68], "float32"),
-    "t4": ("sbuf", [128, 68], "float32"), "t5": ("sbuf", [128, 68], "float32"), "m16": ("sbuf", [128, 4], "float32"),
-    "a1": ("sbuf", [128, 36], "float32"), "a2": ("sbuf", [128, 36], "float32"), "a3": ("sbuf", [128, 36], "float32"),
-    "dif": ("sbuf", [128, 36], "float16"), "e4": ("sbuf", [128, 576], "float16"),
+    "i8": ("sbuf", [128, 8], "float32"), "ig": ("sbuf", [128, 128], "float32"), "it": ("sbuf", [128, 256], "float32"),
+    "ip": ("sbuf", [128, 192], "float32"), "iz": ("sbuf", [128, 64], "float32"), "ir": ("sbuf", [128, 64], "float32"),
+    "ie": ("sbuf", [128, 576], "float32"), "m4": ("sbuf", [128, 4], "float32"), "hb": ("sbuf", [128, 4], "float32"), "xb": ("sbuf", [128, 4], "float32"),
+    "gm8": ("sbuf", [128, 8], "float32"), "bones": ("sbuf", [128, 128], "bfloat16"), "turn": ("sbuf", [128, 256], "float16"),
+    "reset": ("sbuf", [128, 192], "float32"), "sel": ("sbuf", [128, 192], "float16"), "selx": ("sbuf", [128, 192], "float16"),
+    "t1": ("sbuf", [128, 64], "float32"), "t2": ("sbuf", [128, 64], "float32"), "t3": ("sbuf", [128, 64], "float32"),
+    "t4": ("sbuf", [128, 64], "float32"), "t5": ("sbuf", [128, 64], "float32"), "t6": ("sbuf", [128, 64], "float32"),
+    "t7": ("sbuf", [128, 64], "float32"), "e4": ("sbuf", [128, 576], "float16"),
 }
 for _b in range(8):
     SCRATCH["ps%d" % _b] = ("psum", [128, 512], "float32")
-SEMAPHORES = (["cV", "cS", "cP", "cG", "ldq", "ldb", "lde", "ldn", "ldk", "ldk2", "ldv", "sent", "qarr", "bla"]
-              + ["la%d_%d" % (s, h) for s in range(3) for h in range(MAXS)]
-              + ["aa%d" % s for s in range(3)] + ["fa%d" % h for h in range(MAXS)] + ["st%d" % h for h in range(MAXS)])
+SEMAPHORES = (["cV", "cS", "cP", "cG", "ldq", "ldb", "lde", "ldn", "ldk", "ldk2", "ldv", "sent", "qarr", "bla", "qbd"]
+              + ["la%d_%d" % (s, h) for s in range(3) for h in range(NS)]
+              + ["aa%d" % s for s in range(3)] + ["fa%d" % h for h in range(NS)] + ["st%d" % h for h in range(NS)])
 
 
 def build(g, core, T, topo):
     A, F = AluOpType, ActivationFunctionType
-    NS = len(SUBS)
     rank = T.rank_of(core)
     nxt, prv = T.cores[(rank + 1) % N], T.cores[(rank - 1) % N]
     rid, pid, _se = topo.addr(nxt)
     mask = topo.mask(core, nxt)
     n_out, n_in = len(topo.engines(core, nxt)), len(topo.engines(prv, core))
     V, Sc, P, Y = g.vector, g.scalar, g.tensor, g.sync
-    ops, banks, sent, lead = [], {}, [0], [0]
+    ops, sent, lead = [], [0], [0.0]
+    cy = COST["cycle"]
+    dur = lambda n: max(64, n) * cy
+    gdur = lambda n, q: (0.05 if q == "V" else 0.065) + COST["gather"] * n * cy
 
-    def op(q, kind, n, needs, emit, sig=None, bank=None, tag=None, alt=None):
-        needs = [x for x in needs if x is not None]
-        if bank is not None:
-            st = banks.setdefault(bank, [q, [], []])
-            if st[0] != q:
-                st[0], st[2], st[1] = q, st[1], []
-            needs = needs + st[2]
-            st[1].append(len(ops))
-        ops.append([q, kind, n, sorted(set(needs)), emit, sig, lead[0], tag, alt])
+    def op(forms, needs, sig=None, kind="c", nbytes=0):
+        ops.append(dict(forms=forms, needs=sorted(set(x for x in needs if x is not None)), sig=sig, kind=kind, bytes=nbytes, after=[], boost=lead[0]))
         return len(ops) - 1
-
-    def either(e, fv, fs, needs, bank=None, tag=None):
-        if len(ops) in FLIP: e = "S" if e == "V" else "V"
-        a, b = (fv, fs) if e == "V" else (fs, fv)
-        return op(e, a[0], a[1], needs, a[2], bank=bank, tag=tag, alt=("S" if e == "V" else "V", b[0], b[1]))
-    def copy(e, out, a, needs, n, kind="c", bank=None, tag=None):
-        return either(e, (kind, n, lambda: V.tensor_copy(out, a)), (kind, n, lambda: Sc.activation(out, a, F.Copy)), needs, bank, tag)
-    def ts(out, in0, s1, s2, o0, o1, needs, n, bank=None):
-        if o1 is None: return op("V", "c", n, needs, lambda: V.tensor_scalar(out, in0, s1, None, o0), bank=bank)
-        return op("V", "c", n, needs, lambda: V.tensor_scalar(out, in0, s1, s2, o0, o1), bank=bank)
-    def tt(out, a, b, o, needs, n, kind="c", bank=None):
-        return op("V", kind, n, needs, lambda: V.tensor_tensor(out, a, b, o), bank=bank)
-    def cp(out, a, needs, n, kind="c"):
-        return op("V", kind, n, needs, lambda: V.tensor_copy(out, a))
-    def scan(out, d0, d1, o0, o1, needs, n, bank=None):
-        return op("V", "c", n, needs, lambda: V.tensor_tensor_scan(out, d0, d1, 0.0, o0, o1), bank=bank)
-    def mm(lst, needs, bank, tag=None, add=False):
+    def vec(d, emit, needs):
+        return op([("V", d, emit)], needs)
+    def affine(on, out, a, needs, n, add=None, mul=None):
+        d = lambda q: gdur(-n, q) if n < 0 else dur(n)
+        if add is not None:
+            fv, fs = (lambda: V.tensor_scalar(out, a, add, None, A.add)), (lambda: Sc.activation(out, a, F.Identity, bias=add))
+        elif mul is not None:
+            fv, fs = (lambda: V.tensor_scalar(out, a, mul, None, A.mult)), (lambda: Sc.activation(out, a, F.Identity, scale=mul))
+        else:
+            fv, fs = (lambda: V.tensor_copy(out, a)), (lambda: Sc.activation(out, a, F.Copy))
+        return op([(q, d(q), fv if q == "V" else fs) for q in on], needs)
+    def ts(out, in0, s1, s2, o0, o1, needs, n):
+        if o1 is None: return vec(dur(n), lambda: V.tensor_scalar(out, in0, s1, None, o0), needs)
+        return vec(dur(n), lambda: V.tensor_scalar(out, in0, s1, s2, o0, o1), needs)
+    def tt(out, a, b, o, needs, n):
+        return vec(gdur(-n, "V") if n < 0 else dur(n), lambda: V.tensor_tensor(out, a, b, o), needs)
+    def cp(out, a, needs, n):
+        return affine("V", out, a, needs, n)
+    def fill(out, x, needs, n):
+        return vec(dur(n), lambda: V.memset(out, x), needs)
+    def mm(lst, needs, add=False, start=True, stop=True):
         def emit():
-            for x, (o, l, r) in enumerate(lst): ins = P.matmul(o, l, r, x == 0 or not add, x == len(lst) - 1 or not add)
+            for x, (o, l, r) in enumerate(lst):
+                ins = P.matmul(o, l, r, start and (x == 0 or not add), stop and (x == len(lst) - 1 or not add))
             return ins
-        return op("P", "p", sum(max(min(64, l.shape[-1]), r.shape[-1]) for (o, l, r) in lst), needs, emit, bank=bank, tag=tag)
+        return op([("P", COST["pe"] * sum(max(min(64, l.shape[-1]), r.shape[-1]) for (o, l, r) in lst), emit)], needs)
     def iota(out, pat, cm, n, base=0):
-        return op("G", "i", n, [], lambda: g.iota(out, pat, base, cm, allow_small_or_imprecise_dtypes=True))
-    def dma(q, out, in_, sem, n, needs=()):
+        return op([("G", 0.13 + 2 * n * cy, lambda: g.iota(out, pat, base, cm, allow_small_or_imprecise_dtypes=True))], [])
+    def dma(q, pairs, sem, nbytes, needs=()):
         e = Y if q == "Y" else Sc
-        return op(q, "d", n, list(needs), lambda: e.dma_start(out, in_), sig=(sem, 16))
-    def send(emit, needs, sem, cnt, n_loc, n, after=()):
+        def emit():
+            for out, in_ in pairs[:-1]: e.dma_start(out, in_).then_inc(T.sem[sem], 16)
+            return e.dma_start(*pairs[-1])
+        return op([(q, 0.05 * len(pairs), emit)], list(needs), sig=(sem, 16 * len(pairs)), kind="d", nbytes=nbytes)
+    def send(emit, needs, sem, cnt, n_loc, nbytes):
         sent[0] += n_loc
-        a = op("G", "r", 2000 if sem == "qarr" else 0, needs, emit, sig=("sent", None))
-        return op(None, "a", n, [a] + list(after), None, sig=(sem, cnt))
+        a = op([("G", COST["issue"], emit)], needs, sig=("sent", None), kind="r", nbytes=nbytes)
+        return op([], [a], sig=(sem, cnt), kind="a")
 
-    qs = lambda r, a=0, b=Q: T.qall[:, r * Q + a:r * Q + b]
-    lead[0] = -1
-    ldq = dma("Y", qs(rank), T.q[:], "ldq", 4e4)
-    ldb = dma("S", T.brs[0:32, :], T.br[:], "ldb", 14e4)
-    lde = dma("S", T.ent[:], T.entry[:], "lde", 16e4)
-    lead[0] = 0
-    ldn = dma("Y", T.nbw[:], T.nb[:], "ldn", 176e4)
-    ldk = dma("S", T.kw[:, 0:KA], T.k[:, 0:KA], "ldk", 256e4)
+    qs = lambda s, a=0, b=Q: T.qall[:, s * Q + a:s * Q + b]
+    ldb = dma("S", [(T.brs[0:32, :], T.br[:])], "ldb", 4 * 8 * S)
+    ldq = dma("Y", [(qs(0), T.q[:])], "ldq", 256 * Q)
+    lde = dma("S", [(T.ent[:], T.entry[:])], "lde", 4096)
+    ldn = dma("Y", [(T.nbw[:], T.nb[:])], "ldn", 512 * S)
+    ldk = dma("S", [(T.kw[:, 0:KA], T.k[:, 0:KA])], "ldk", 256 * KA) if KA else None
+    ops[ldn]["after"], ops[lde]["after"] = [ldb, ldq, lde], [ldb]
+    if KA: ops[ldk]["after"] = [ldn]
 
     others = [c for c in T.cores if c != core]
     def qmask(c):
@@ -112,125 +113,124 @@ def build(g, core, T, topo):
     bits = lambda m: bin(m).count("1")
     def qsend():
         ids = [DstId(rid=topo.addr(d)[0], pnc=topo.addr(d)[1]) for d in others]
-        tr = RemoteDMATransfer(dst_ids=ids, dma_engine_mask=qmask(core), remote_sem=T.sem.qarr, srcs=[qs(rank)], dsts=[qs(rank)] * len(others))
+        dsts = [qs((T.rank_of(d) - rank) % N) for d in others]
+        tr = RemoteDMATransfer(dst_ids=ids, dma_engine_mask=qmask(core), remote_sem=T.sem.qarr, srcs=[qs(0)], dsts=dsts)
         return g.remote_dma_fused([tr], local_sem=T.sem.sent)
 
-    gp = op("G", "i", 1, [], lambda: g.iota(T.pi[:, 0:1], [[0, 1]], 0, 1))
+    n3 = 48 * W
+    gp = op([("G", 0.13, lambda: g.iota(T.pi[:, 0:1], [[0, 1]], 0, 1))], [])
     g8 = iota(T.i8[:], [[1, 8]], 0, 8)
     ge = iota(T.ie[0:32, :], [[4, 4], [1, 144]], -4, 576, -15)
-    g17 = iota(T.i17[:], [[0, 4], [1, 17]], 0, 68)
-    gz = iota(T.iz[:], [[32, 4], [1, 17]], -1, 68)
-    gu = iota(T.iu[:, 0:34], [[16, 2], [1, 17]], 0, 34)
-    gg = iota(T.ig[:], [[1, 8], [0, 16]], 0, 128)
-    qarr = send(qsend, [ldq, gp, g8, ge, g17, gz, gu, gg], "qarr", sum(bits(qmask(c)) for c in others), bits(qmask(core)), 0, [ldn])
+    gi = iota(T.ip[:, 0:n3], [[0, 3 * W], [1, 16]], 0, n3)
+    gz = iota(T.iz[:, 0:16 * W], [[32, W], [1, 16]], -1, 16 * W)
+    gr = iota(T.ir[:, 0:16 * W], [[32, W], [0, 16]], -1, 16 * W, 16)
+    gt = iota(T.it[:], [[16, 8], [0, 2], [1, 16]], -1, 256)
+    qarr = send(qsend, [ldq], "qarr", sum(bits(qmask(c)) for c in others), bits(qmask(core)), 3 * 256 * Q)
     b0 = ts(T.pb[:, 0:1], T.pi[:, 0:1], 3, None, A.bitwise_and, None, [gp], 1)
-    b1 = ts(T.pb[:, 1:2], T.pi[:, 0:1], 31, None, A.bitwise_and, None, [gp], 1)
+    b1 = ts(T.pb[:, 1:2], T.pi[:, 0:1], 16, None, A.bitwise_and, None, [gp], 1)
     b2 = ts(T.pb[:, 2:3], T.pi[:, 0:1], 4, None, A.arith_shift_right, None, [gp], 1)
     pf = cp(T.pf[:, 0:3], T.pb[:, 0:3], [b0, b1, b2], 3)
-    p3, p31, pg = T.pf[:, 0:1], T.pf[:, 1:2], T.pf[:, 2:3]
-    hb = op("V", "c", 1, [], lambda: V.memset(T.hb[:], -float(HALF)))
+    p3, p16, pg = T.pf[:, 0:1], T.pf[:, 1:2], T.pf[:, 2:3]
+    hb = fill(T.hb[:], -float(HALF), [], 4)
+    xb = ts(T.xb[:, 0:1], p16, (32768.0 + HALF) / 16, None, A.mult, None, [pf], 1)
     gm8 = ts(T.gm8[:], T.i8[:], pg, None, A.is_equal, None, [pf, g8], 8)
-    bones = ts(T.bones[:], T.ig[:], pg, None, A.is_equal, None, [pf, gg], 128)
     m4 = ts(T.m4[:], T.i8[:, 0:4], p3, None, A.is_equal, None, [pf, g8], 4)
-    reset = ts(T.reset[:], T.i17[:], 0.0, -1000000.0, A.is_equal, A.mult, [g17], 68)
-    m16 = ts(T.m16[:, 0:1], T.pi[:, 0:1], 16.0, None, A.is_equal, None, [gp], 1)
-    t1 = ts(T.t1[:], T.iz[:], 0.0, 16.0, A.is_equal, A.mult, [gz], 68)
-    t2 = ts(T.t2[:], T.i17[:], 16.0, -30000.0, A.is_equal, A.mult, [g17], 68)
-    t3 = ts(T.t3[:], T.i17[:], -1.0, 15.0, A.mult, A.add, [g17], 68)
-    t4 = tt(T.t4[:], T.t3[:], T.t2[:], A.add, [t2, t3], 136)
-    t5 = ts(T.t5[:], T.t4[:], T.m16[:, 0:1], None, A.mult, None, [t4, m16], 68)
-    sel = tt(T.sel[:], T.t5[:], T.t1[:], A.add, [t5, t1], 136)
-    a1 = ts(T.a1[:, 0:34], T.iu[:, 0:34], -1.0, p31, A.add, A.is_equal, [gu, pf], 34)
-    a2 = ts(T.a2[:, 0:34], T.iu[:, 0:34], p31, None, A.is_equal, None, [gu, pf], 34)
-    a3 = ts(T.a3[:, 0:34], T.i17[:, 0:34], 16.0, None, A.not_equal, None, [g17], 34)
-    a4 = tt(T.a2[:, 0:34], T.a2[:, 0:34], T.a3[:, 0:34], A.mult, [a2, a3], 68)
-    dif = tt(T.dif[:, 0:34], T.a1[:, 0:34], T.a2[:, 0:34], A.subtract, [a1, a4], 68)
+    turn = ts(T.turn[:], T.it[:], 0.0, None, A.is_equal, None, [gt], 256)
+    reset = ts(T.reset[:, 0:n3], T.ip[:, 0:n3], 0.0, -1e9, A.is_equal, A.mult, [gi], n3)
+    n1 = 16 * W
+    t = [T["t%d" % x][:, 0:n1] for x in range(1, 8)]
+    seg = lambda b, x: b[:, n1 * x:n1 * x + n1]
+    e0 = ts(t[0], T.iz[:, 0:n1], 0.0, None, A.is_equal, None, [gz], n1)
+    e16 = ts(t[1], T.iz[:, 0:n1], -16.0, None, A.is_equal, None, [gz], n1)
+    r16 = ts(t[2], T.ir[:, 0:n1], 0.0, None, A.is_equal, None, [gr], n1)
+    u = ts(t[3], T.ip[:, 0:n1], -1.0, 15.0, A.mult, A.add, [gi], n1)
+    ur = tt(t[4], t[3], t[2], A.mult, [u, r16], 2 * n1)
+    base = tt(t[5], t[4], t[0], A.add, [ur, e0], 2 * n1)
+    rh = ts(t[6], t[2], -float(HALF), None, A.mult, None, [r16], n1)
+    s2 = ts(t[3], t[5], C_LO + C_HI, None, A.mult, None, [base], n1)
+    sel = [ts(seg(T.sel, 0), t[5], C_LO, None, A.mult, None, [base], n1), ts(seg(T.sel, 1), t[5], C_HI, None, A.mult, None, [base], n1),
+           tt(seg(T.sel, 2), t[3], t[6], A.add, [s2, rh], 2 * n1)]
+    selx = [tt(seg(T.selx, 0), t[0], t[1], A.subtract, [e0, e16], 2 * n1), cp(seg(T.selx, 1), t[1], [e16], n1),
+            ts(seg(T.selx, 2), t[1], 0.0, None, A.mult, None, [e16], n1)]
     e4 = [ts(T.e4[0:32, 144 * x:144 * x + 144], T.ie[0:32, 144 * x:144 * x + 144], 0.0, T.m4[0:32, x:x + 1], A.is_equal, A.mult, [ge, m4], 144) for x in range(4)]
-    pad = [ts(T.ch[:, 80 * h:80 * h + 16], T.i17[:, 0:16], 0.0, None, A.mult, None, [g17], 16) for h in range(NS)]
-    PA = [T["ps%d" % h] for h in range(NS)]
-    PK = [T["ps%d" % (NS + h)] for h in range(NS)]
-    own_s = 3 * NS <= 6
-    bS = [2 * NS + h if own_s else h for h in range(NS)]
-    cS = 0 if own_s else 128
+    PA = [T["ps%d" % (2 * h)] for h in range(NS)]
+    PK = [T["ps%d" % (2 * h + 1)] for h in range(NS)]
+    ones = [fill(PA[h][:, 0:128], 1.0 / 16, [], 128) for h in range(NS)]
 
-    brh = ts(T.brh[0:32, :], T.brs[0:32, :], -float(HALF), None, A.add, None, [ldb], 768)
-    bl = [mm([(T.ps7[:, 48 * x:48 * x + 48], T.e4[0:32, 144 * x + 15 - b:144 * x + 143 - b], T.brh[0:32, b::16]) for b in range(16)],
-             [brh, e4[x]], 7, add=True) for x in range(4)]
-    blo = ts(T.blo[:], T.ps7[:, 0:192], float(HALF), None, A.add, None, bl, 192, bank=7)
-    bla = send(lambda: g.remote_dma(T.bli[:], T.blo[:], T.sem.bla, T.sem.sent, pid, rid, mask), [blo, qarr - 1], "bla", n_in, n_out, 0, [ldn])
-    z = 192 // len(NB2)
-    nb2 = [copy(e, T.nb2[:, 16 * z * x:16 * z * (x + 1)], T.nbw[:, :].indirect(T.bli[:, z * x:z * (x + 1)]), [bla, ldn], 16 * z, "g", tag="b")
-           for x, e in enumerate(NB2)]
-    ones = [op("V", "c", 128, [blo], (lambda h=h: V.memset(PA[h][:, 0:128], 1.0)), bank=h) for h in range(NS)]
+    brh = [affine(e, T.brh[0:32, a:a + 384], T.brs[0:32, a:a + 384], [ldb, hb], 384, add=T.hb[0:32, 0:1]) for e, a in (("V", 0), ("S", 384))]
+    PB = PK[0]
+    bl = [mm([(PB[:, 48 * x:48 * x + 48], T.e4[0:32, 144 * x + 15 - b:144 * x + 143 - b], T.brh[0:32, b::16]) for b in range(16)],
+             brh + [e4[x]], add=True) for x in range(4)]
+    blo = ts(T.blo[:], PB[:, 0:192], float(HALF), None, A.add, None, bl, 192)
+    bla = send(lambda: g.remote_dma(T.bli[:], T.blo[:], T.sem.bla, T.sem.sent, pid, rid, mask), [blo, qarr - 1], "bla", n_in, n_out, 384 * 128)
+    gg = iota(T.ig[:], [[1, 8], [0, 16]], 0, 128)
+    ops[gg]["after"] = [bla - 1]
+    bones = ts(T.bones[:], T.ig[:], pg, None, A.is_equal, None, [pf, gg], 128)
+    z = 192 // NB2
+    nb2 = [affine("VS", T.nb2[:, 16 * z * x:16 * z * (x + 1)], T.nbw[:, :].indirect(T.bli[:, z * x:z * (x + 1)]), [bla, ldn], -16 * z) for x in range(NB2)]
 
-    qb = {}
-    for s in range(N):
-        r = (rank - s) % N
-        qb[s] = [ts(T.qblk[:, x * N * Q + r * Q:x * N * Q + r * Q + Q], qs(r), T.gm8[:, x:x + 1], None, A.mult, None,
-                    [gm8] + ([ldq, blo] if s == 0 else [qarr]), 64) for x in range(8)]
+    qb0 = [affine("VS", T.qblk[:, x * N * Q:x * N * Q + Q], qs(0), [gm8, ldq], 64, mul=T.gm8[:, x:x + 1]) for x in range(8)]
+    zero = [fill(T.qblk[:, x * N * Q + Q:(x + 1) * N * Q], 0.0, [], 192) for x in range(8)]
+    qbd = dma("Y", [(T.qblk[16 * x:16 * x + 16, x * N * Q + Q:(x + 1) * N * Q], T.qall[16 * x:16 * x + 16, Q:N * Q]) for x in range(8)],
+              "qbd", 3 * 256 * Q, zero + [qarr])
 
-    ldk2 = dma("Y", T.kw[:, KA:S], T.k[:, KA:S], "ldk2", 52e4, qb[0] + ones)
-    ldv = dma("Y", T.vw[:], T.v[:], "ldv", 79e4, [ldn, ldk, ldk2])
+    ldk2 = dma("Y", [(T.kw[:, KA:S], T.k[:, KA:S])], "ldk2", 256 * (S - KA), [gg])
+    ldv = dma("Y", [(T.vw[:], T.v[:])], "ldv", 256 * S, [ldn, ldk, ldk2])
     slot = [0]
     def newlist(w):
         slot[0] += 1
-        return T.lst[:, 8 * (slot[0] - 1):8 * (slot[0] - 1) + w]
+        return lambda a=0, b=w, o=8 * (slot[0] - 1): T.lst[:, o + a:o + b]
 
     cur = []
     for h, (a0, w) in enumerate(SUBS):
         L = newlist(w)
-        cur.append((L, cp(L, T.ent[:, a0:a0 + w], [lde], 8)))
-    last = [None] * NS
-    accin = None
+        cur.append((L(), [cp(L(), T.ent[:, a0:a0 + w], [lde], 8)]))
+    last = [[] for _h in SUBS]
+    accin, lastrl = None, [None] * NS
     for s in range(N):
-        r = (rank - s) % N
         terms = []
         for h, (a0, w) in enumerate(SUBS):
-            n, m = 16 * w, 17 * w
+            n = 16 * w
             L, rdy = cur[h]
-            lead[0] = NS - h
-            cu, ch, kg = T.cu, T.ch, T.kg
-            c0, h0, k0 = 64 * h, 80 * h, 1024 * h
-            rr, nf, yy = (x[:, 68 * h:68 * h + m] for x in (T.rr, T.nf, T.yy))
-            K, E = PK[h][:, 0:m], PK[h][:, 128:128 + m]
+            lead[0] = COST["lead"] * (NS - 1 - h)
+            c0, k0 = 64 * h, 1024 * h
+            cc, cf = T.cu[:, c0:c0 + n], T.ch[:, c0:c0 + n]
+            B, X = T.bs[0:32 * w, 128 * h:128 * h + 128], T.bx[0:32 * w, 128 * h:128 * h + 128]
+            K, rr = PK[h][:, 0:n3], T.rr[:, 192 * h:192 * h + n3]
             for step in range(2):
                 far = s > 0 and step == 0
-                win = (T.nb2 if far else T.nbw)[:, :].indirect(L)
-                cc, cf = cu[:, c0:c0 + n], ch[:, h0 + 16:h0 + 16 + n]
-                cg = cp(cc, win, [rdy, last[h]] + (nb2 if far else [ldn]), n, "g")
-                c16 = either("V", ("c", n // 2, lambda cf=cf, cc=cc: V.tensor_scalar(cf, cc, -float(HALF), None, A.add)),
-                             ("g", n, lambda cf=cf, win=win: Sc.activation(cf, win, F.Identity, bias=T.hb[:, 0:1])), [cg, pad[h], hb])
-                m1 = mm([(PK[h][32 * G:32 * G + 32, 128 + 17 * a:128 + 17 * a + 17], ch[32 * G:32 * G + 32, h0 + 16 * a:h0 + 16 * a + 32],
-                          T.dif[32 * G:32 * G + 32, 17:34]) for G in range(4) for a in range(w)], [c16, dif], NS + h)
-                m0 = mm([(PK[h][32 * G:32 * G + 16, 128 + 17 * a:128 + 17 * a + 17], ch[32 * G:32 * G + 32, h0 + 16 * a + 16:h0 + 16 * a + 32],
-                          T.dif[32 * G:32 * G + 32, 0:17]) for G in range(4) for a in range(w)], [m1], NS + h)
+                win, have = (T.nb2 if far else T.nbw)[:, :].indirect(L), rdy + last[h] + (nb2 if far else [ldn])
+                cg = cp(cc, win, have, -n)
+                c16 = affine("S", cf, win, have + [hb], -n, add=T.hb[:, 0:1])
+                tu = [mm([(PK[h][32 * c:32 * c + 32, 256 + 16 * x:256 + 16 * x + 16], T.turn[:, 32 * x:32 * x + 32], T.ch[:, c0 + 16 * c:c0 + 16 * c + 16])
+                          for x in range(8)], [c16, turn, blo, lastrl[h]]) for c in range(w)]
+                ex = affine("VS", X, PK[h][0:32 * w, 256:384], tu + [xb], 128, add=T.xb[0:32 * w, 0:1])
+                px = mm([(K, X, T.selx[0:32 * w, 0:n3])], [ex] + selx, stop=False)
                 pe1, j0 = [], 0
-                for x, (e, cnt) in enumerate(zip(ENG, PIECES[(s * NS + h) * 2 + step])):
-                    tag = ((s * NS + h) * 2 + step, x)
-                    ga = copy(e, kg[:, k0 + 16 * j0:k0 + 16 * (j0 + cnt)], T.kw[:, :].indirect(cu[:, c0 + j0:c0 + j0 + cnt]), [cg, ldk, ldk2], 16 * cnt, "g", tag=tag)
-                    pe1.append(mm([(PA[h][32 * (j // 16):32 * (j // 16) + 16, (j % 16):128:16], kg[:, k0 + 16 * j:k0 + 16 * j + 16],
-                                    T.qblk[:, r * Q + 16 * a0 + j::N * Q]) for j in range(j0, j0 + cnt)], [ga] + qb[s] + [ones[h]], h, tag))
+                for cnt in PIECES[w]:
+                    ga = affine("VS", T.kg[:, k0 + 16 * j0:k0 + 16 * (j0 + cnt)], T.kw[:, :].indirect(T.cu[:, c0 + j0:c0 + j0 + cnt]), [cg, ldk, ldk2], -16 * cnt)
+                    pe1.append(mm([(PA[h][32 * (j // 16):32 * (j // 16) + 16, (j % 16):128:16], T.kg[:, k0 + 16 * j:k0 + 16 * j + 16],
+                                    T.qblk[:, s * Q + 16 * a0 + j::N * Q]) for j in range(j0, j0 + cnt)], [ga, ones[h]] + (qb0 if s == 0 else [qbd])))
                     j0 += cnt
-                B = T.bsb[0:32 * w, 128 * h:128 * h + 128]
-                ev = copy("V", B, PA[h][0:32 * w, 0:128], pe1, 128, bank=h)
-                p2 = mm([(K, B, T.sel[0:32 * w, 0:m])], [ev, sel], NS + h)
-                s1 = scan(rr, T.reset[:, 0:m], K, A.add, A.max, [p2, reset], m, bank=NS + h)
-                lt = tt(nf, K, rr, A.is_lt, [s1], m, bank=NS + h)
-                s2 = scan(yy, E, nf, A.add, A.mult, [lt, m0], m, bank=NS + h)
-                L = newlist(w)
-                rdy = ts(L, T.yy[:, 68 * h + 16:68 * h + m:17], float(HALF), None, A.add, None, [s2], w)
+                ev = affine("VS", B, PA[h][0:32 * w, 0:128], pe1, 128, mul=16.0)
+                p2 = mm([(K, B, T.sel[0:32 * w, 0:n3])], [ev, px] + sel, start=False)
+                sc = vec(dur(n3), (lambda rr=rr, K=K: V.tensor_tensor_scan(rr, T.reset[:, 0:n3], K, 0.0, A.add, A.max)), [p2, reset])
+                Ln = newlist(w)
+                top = lambda x, c: T.rr[:, 192 * h + n1 * x + 16 * c + 15:192 * h + n1 * x + 16 * c + 16]
+                rdy = [ts(Ln(c, c + 1), top(1, c), top(2, c), top(0, c), A.subtract, A.add, [sc], 1) for c in range(w)]
+                L = Ln()
                 last[h] = rdy
             x0 = s * Q + 16 * a0
             if s < N - 1:
                 Li = T.lin[:, 8 * (s * NS + h):8 * (s * NS + h) + w]
                 sem = "la%d_%d" % (s, h)
-                cur[h] = (Li, send((lambda Li=Li, L=L, sem=sem: g.remote_dma(Li, L, T.sem[sem], T.sem.sent, pid, rid, mask)), [rdy], sem, n_in, n_out, 0))
-            kq = tt(T.kq[:, x0:x0 + n], T.kw[:, :].indirect(L), qs(r, 16 * a0, 16 * a0 + n), A.mult, [rdy, ldq if s == 0 else qarr], n, "g")
-            ps, rs = T["ps%d" % bS[h]][:, cS:cS + n], T.rs[:, x0:x0 + n]
-            sm = mm([(ps, T.bones[:], T.kq[:, x0:x0 + n])], [kq, bones], bS[h])
-            rl = either("S", ("c", n, lambda rs=rs, ps=ps: V.tensor_scalar(rs, ps, 0.0, None, A.max)),
-                        ("c", n, lambda rs=rs, ps=ps: Sc.activation(rs, ps, F.Relu)), [sm], bank=bS[h])
-            terms.append(tt(T.term[:, x0:x0 + n], T.vw[:, :].indirect(L), rs, A.mult, [rl, ldv], n, "g"))
+                cur[h] = (Li, [send((lambda Li=Li, L=L, sem=sem: g.remote_dma(Li, L, T.sem[sem], T.sem.sent, pid, rid, mask)), rdy, sem, n_in, n_out, 1024)])
+            kq = tt(T.kq[:, x0:x0 + n], T.kw[:, :].indirect(L), qs(s, 16 * a0, 16 * a0 + n), A.mult, rdy + [ldq if s == 0 else qarr], -n)
+            ps, rs = PK[h][:, 384:384 + n], T.rs[:, x0:x0 + n]
+            sm = mm([(ps, T.bones[:], T.kq[:, x0:x0 + n])], [kq, bones])
+            lastrl[h] = op([("V", dur(n), lambda rs=rs, ps=ps: V.tensor_scalar(rs, ps, 0.0, None, A.max)),
+                            ("S", dur(n), lambda rs=rs, ps=ps: Sc.activation(rs, ps, F.Relu))], [sm])
+            terms.append(tt(T.term[:, x0:x0 + n], T.vw[:, :].indirect(L), rs, A.mult, [lastrl[h], ldv], -n))
 
         def accsend(a, b, sem, s=s):
             dst, src = T.acc[:, s * Q + a:s * Q + b], T.term[:, s * Q + a:s * Q + b]
@@ -239,33 +239,83 @@ def build(g, core, T, topo):
                                    srcs=[src, T.acc[:, (s - 1) * Q + a:(s - 1) * Q + b]], dsts=[dst], alu_op=1)
             return g.remote_dma_fused([tr], local_sem=T.sem.sent)
         if s < N - 1:
-            accin = send((lambda f=accsend, s=s: f(0, Q, "aa%d" % s)), terms + [accin], "aa%d" % s, n_in, n_out, 13e4)
+            accin = send((lambda f=accsend, s=s: f(0, Q, "aa%d" % s)), terms + [accin], "aa%d" % s, n_in, n_out, 1024 * Q)
         else:
             for h, (a0, w) in enumerate(SUBS):
                 a, b = 16 * a0, 16 * (a0 + w)
                 fa = send((lambda f=accsend, a=a, b=b, h=h: f(a, b, "fa%d" % h)), [terms[h], accin], "fa%d" % h, n_in, n_out, 16384 * w)
-                dma("Y", T.y[:, a:b], T.acc[:, s * Q + a:s * Q + b], "st%d" % h, 8192 * w, [fa])
+                dma("Y", [(T.y[:, a:b], T.acc[:, s * Q + a:s * Q + b])], "st%d" % h, 8192 * w, [fa])
     return ops, sent[0]
+
+
+def schedule(ops):
+    wait = COST["wait"]
+    lat = lambda o: {"d": COST["dma"] + o["bytes"] / COST["rate"], "r": COST["remote"] + o["bytes"] / COST["rate"]}.get(o["kind"], 0.0)
+    way, users = [0.0] * len(ops), [[] for _o in ops]
+    for i, o in enumerate(ops):
+        for d in o["needs"] + o["after"]: users[d].append(i)
+    for i in reversed(range(len(ops))):
+        o = ops[i]
+        way[i] = max([way[u] for u in users[i]] + [0.0]) + (min(f[1] for f in o["forms"]) + lat(o) + wait if o["forms"] else 0.0)
+    way = [x + o["boost"] for x, o in zip(way, ops)]
+    free, pipe, first = {q: 0.0 for q in "VSPGY"}, [0.0], [COST["first"]]
+    done, began, left, order = {}, {}, [len(o["needs"] + o["after"]) for o in ops], []
+    ready = [i for i, o in enumerate(ops) if not left[i]]
+    while ready:
+        cand = []
+        for i in ready:
+            at = max([done[d] for d in ops[i]["needs"]] + [began[d] for d in ops[i]["after"]] + [0.0])
+            can = [(max(at, free[f[0]]), i, x, f[0], f[1]) for x, f in enumerate(ops[i]["forms"])]
+            if len(can) == 2 and can[1][0] <= can[0][0] + COST["spare"]: can = can[1:]
+            cand += can or [(-1.0, i, None, None, 0.0)]
+        cand.sort(key=lambda c: (c[0], -way[c[1]], c[4]))
+        def holds_up(c):
+            for e in cand:
+                if e[0] >= c[0] + c[4]: return False
+                if e[3] == c[3] and way[e[1]] > way[c[1]] + COST["margin"] and c[0] + c[4] - e[0] > COST["look"] * (e[0] - c[0]):
+                    if not any(z[1] == e[1] and z[3] != e[3] and z[0] <= e[0] for z in cand): return True
+            return False
+        t, i, x, q, d = next(c for c in cand if not holds_up(c))
+        o = ops[i]
+        began[i] = t
+        if x is None:
+            done[i] = done[o["needs"][0]]
+        else:
+            if o["kind"] == "r": d, first[0] = d + first[0], 0.0
+            free[q] = t + d
+            done[i] = t + d + wait
+            if o["kind"] in "dr":
+                half = (lat(o) - o["bytes"] / COST["rate"]) / 2
+                pipe[0] = max(pipe[0], t + d + half) + o["bytes"] / COST["rate"]
+                done[i] = pipe[0] + half + wait
+        order.append((i, x))
+        ready.remove(i)
+        for u in users[i]:
+            left[u] -= 1
+            if left[u] == 0: ready.append(u)
+    return order
 
 
 def rank_program(g, core, T, topo):
     if T.rank_of(core) is None:
         return
     ops, sent = build(g, core, T, topo)
-    pos = {i: x for x, i in enumerate(ORDER)}
+    order = schedule(ops)
+    pos = {i: x for x, (i, _f) in enumerate(order)}
     queue = {"V": g.vector, "S": g.scalar, "P": g.tensor, "G": g, "Y": g.sync}
     count = {"cV": 0, "cS": 0, "cP": 0, "cG": 0}
     known = {q: {} for q in queue}
     sig, clock, stores = {}, {}, []
-    for i in ORDER:
-        q, needs, emit, sg = ops[i][0], ops[i][3], ops[i][4], ops[i][5]
-        if q is None:
+    for i, x in order:
+        needs, sg = ops[i]["needs"], ops[i]["sig"]
+        if x is None:
             sig[i], clock[i] = sg, {sg[0]: sg[1]}
             continue
+        q, _d, emit = ops[i]["forms"][x]
         kn = known[q]
         for d in sorted(needs, key=lambda d: -pos[d]):
             sem, cnt = sig[d]
-            if kn.get(sem, 0) >= cnt: continue
+            if kn.get(sem, 0) >= cnt or (q == "P" and sem == "cP"): continue
             queue[q].wait_ge(T.sem[sem], cnt)
             for k2, v2 in clock[d].items():
                 if kn.get(k2, 0) < v2: kn[k2] = v2
@@ -278,7 +328,7 @@ def rank_program(g, core, T, topo):
         elif sg[1] is None:
             sig[i] = (sg[0], 0)
         else:
-            ins.then_inc(T.sem[sg[0]], sg[1])
+            ins.then_inc(T.sem[sg[0]], 16)
             sig[i] = sg
             if sg[0].startswith("st"): stores.append(sg)
         clock[i] = dict(kn)

@@ -3,13 +3,14 @@ from concourse.mybir import AluOpType, ActivationFunctionType
 
 S, Q, N = 3072, 128, 4
 HALF = S // 2
-SUBS = [(0, 3), (3, 3), (6, 2)]
-NS, W = len(SUBS), max(w for _a, w in SUBS)
-PIECES = {4: [20, 20, 12, 12], 3: [16, 16, 8, 8], 2: [12, 12, 8]}
-KA = 1024
-NB2 = 8
-C_LO, C_HI = 64.0, 4096.0
-COST = dict(cycle=0.00092, gather=1.5, pe=0.00046, wait=0.2, dma=1.0, rate=3e5, issue=0.3, first=2.0, remote=1.2, look=0.5, margin=0.2, spare=0.1, lead=0.6)
+NS, W = 4, 2
+PIECES = [18, 14]
+TERMS = [[0, 1, 2, 3]]
+TAILS = [[0, 1], [2, 3]]
+KA = 3072
+NB2 = 16
+C_LO, C_HI = 64.0, 3200.0
+COST = dict(cycle=0.00088, gather=1.4, pe=0.00046, wait=0.25, dma=1.0, rate=4e5, issue=0.3, first=2.0, remote=1.2, look=0.5, margin=0.2, spare=0.1, lead=0.4)
 
 SCRATCH = {
     "nbw": ("sbuf", [128, S], "int32"), "kw": ("sbuf", [128, S], "bfloat16"), "vw": ("sbuf", [128, S], "bfloat16"),
@@ -17,10 +18,10 @@ SCRATCH = {
     "brs": ("sbuf", [128, 768], "int32"), "brh": ("sbuf", [128, 768], "float16"),
     "qall": ("sbuf", [128, N * Q], "bfloat16"), "qblk": ("sbuf", [128, 8 * N * Q], "bfloat16"),
     "ent": ("sbuf", [128, 8], "int32"),
-    "lst": ("sbuf", [128, 8 * 9 * NS], "uint16"), "lin": ("sbuf", [128, 8 * 3 * NS], "uint16"),
-    "cu": ("sbuf", [128, 64 * NS], "uint16"), "ch": ("sbuf", [128, 64 * NS], "float16"),
-    "kg": ("sbuf", [128, 1024 * NS], "bfloat16"), "bs": ("sbuf", [128, 128 * NS], "float16"), "bx": ("sbuf", [128, 128 * NS], "float16"),
-    "rr": ("sbuf", [128, 192 * NS], "float32"),
+    "lst": ("sbuf", [128, 8 * 9], "uint16"), "lin": ("sbuf", [128, 8 * 3 * NS], "uint16"),
+    "cu": ("sbuf", [128, Q], "uint16"), "ch": ("sbuf", [128, Q], "float16"),
+    "kg": ("sbuf", [128, 16 * Q], "bfloat16"), "bs": ("sbuf", [128, 128 * NS], "float16"),
+    "rr": ("sbuf", [128, 96 * NS], "float32"),
     "kq": ("sbuf", [128, N * Q], "bfloat16"), "rs": ("sbuf", [128, N * Q], "float32"),
     "term": ("sbuf", [128, N * Q], "float32"), "acc": ("sbuf", [128, N * Q], "float32"),
     "pi": ("sbuf", [128, 4], "int32"), "pb": ("sbuf", [128, 4], "int32"), "pf": ("sbuf", [128, 4], "float32"),
@@ -28,16 +29,14 @@ SCRATCH = {
     "ip": ("sbuf", [128, 192], "float32"), "iz": ("sbuf", [128, 64], "float32"), "ir": ("sbuf", [128, 64], "float32"),
     "ie": ("sbuf", [128, 576], "float32"), "m4": ("sbuf", [128, 4], "float32"), "hb": ("sbuf", [128, 4], "float32"), "xb": ("sbuf", [128, 4], "float32"),
     "gm8": ("sbuf", [128, 8], "float32"), "bones": ("sbuf", [128, 128], "bfloat16"), "turn": ("sbuf", [128, 256], "float16"),
-    "reset": ("sbuf", [128, 192], "float32"), "sel": ("sbuf", [128, 192], "float16"), "selx": ("sbuf", [128, 192], "float16"),
-    "t1": ("sbuf", [128, 64], "float32"), "t2": ("sbuf", [128, 64], "float32"), "t3": ("sbuf", [128, 64], "float32"),
-    "t4": ("sbuf", [128, 64], "float32"), "t5": ("sbuf", [128, 64], "float32"), "t6": ("sbuf", [128, 64], "float32"),
-    "t7": ("sbuf", [128, 64], "float32"), "e4": ("sbuf", [128, 576], "float16"),
+    "reset": ("sbuf", [128, 96], "float32"), "sel": ("sbuf", [128, 96], "float16"),
+    "tmp": ("sbuf", [128, 32 * 12], "float32"), "e4": ("sbuf", [128, 576], "float16"),
 }
-for _b in range(8):
+for _b in range(NS + 2):
     SCRATCH["ps%d" % _b] = ("psum", [128, 512], "float32")
 SEMAPHORES = (["cV", "cS", "cP", "cG", "ldq", "ldb", "lde", "ldn", "ldk", "ldk2", "ldv", "sent", "qarr", "bla", "qbd"]
               + ["la%d_%d" % (s, h) for s in range(3) for h in range(NS)]
-              + ["aa%d" % s for s in range(3)] + ["fa%d" % h for h in range(NS)] + ["st%d" % h for h in range(NS)])
+              + ["aa%d" % s for s in range(3)] + ["fa%d" % h for h in range(len(TAILS))] + ["st%d" % h for h in range(len(TAILS))])
 
 
 def build(g, core, T, topo):
@@ -122,43 +121,42 @@ def build(g, core, T, topo):
     g8 = iota(T.i8[:], [[1, 8]], 0, 8)
     ge = iota(T.ie[0:32, :], [[4, 4], [1, 144]], -4, 576, -15)
     gi = iota(T.ip[:, 0:n3], [[0, 3 * W], [1, 16]], 0, n3)
-    gz = iota(T.iz[:, 0:16 * W], [[32, W], [1, 16]], -1, 16 * W)
-    gr = iota(T.ir[:, 0:16 * W], [[32, W], [0, 16]], -1, 16 * W, 16)
+    gz = iota(T.iz[:, 0:16 * W], [[64, W], [1, 16]], -1, 16 * W)
+    gr = iota(T.ir[:, 0:16 * W], [[64, W], [0, 16]], -1, 16 * W, 16)
     gt = iota(T.it[:], [[16, 8], [0, 2], [1, 16]], -1, 256)
     qarr = send(qsend, [ldq], "qarr", sum(bits(qmask(c)) for c in others), bits(qmask(core)), 3 * 256 * Q)
     b0 = ts(T.pb[:, 0:1], T.pi[:, 0:1], 3, None, A.bitwise_and, None, [gp], 1)
-    b1 = ts(T.pb[:, 1:2], T.pi[:, 0:1], 16, None, A.bitwise_and, None, [gp], 1)
+    b1 = ts(T.pb[:, 1:2], T.pi[:, 0:1], 48, None, A.bitwise_and, None, [gp], 1)
     b2 = ts(T.pb[:, 2:3], T.pi[:, 0:1], 4, None, A.arith_shift_right, None, [gp], 1)
     pf = cp(T.pf[:, 0:3], T.pb[:, 0:3], [b0, b1, b2], 3)
-    p3, p16, pg = T.pf[:, 0:1], T.pf[:, 1:2], T.pf[:, 2:3]
+    p3, p48, pg = T.pf[:, 0:1], T.pf[:, 1:2], T.pf[:, 2:3]
     hb = fill(T.hb[:], -float(HALF), [], 4)
-    xb = ts(T.xb[:, 0:1], p16, (32768.0 + HALF) / 16, None, A.mult, None, [pf], 1)
+    xb = ts(T.xb[:, 0:1], p48, 48.0, 32768.0 + HALF, A.is_equal, A.mult, [pf], 1)
     gm8 = ts(T.gm8[:], T.i8[:], pg, None, A.is_equal, None, [pf, g8], 8)
     m4 = ts(T.m4[:], T.i8[:, 0:4], p3, None, A.is_equal, None, [pf, g8], 4)
     turn = ts(T.turn[:], T.it[:], 0.0, None, A.is_equal, None, [gt], 256)
     reset = ts(T.reset[:, 0:n3], T.ip[:, 0:n3], 0.0, -1e9, A.is_equal, A.mult, [gi], n3)
     n1 = 16 * W
-    t = [T["t%d" % x][:, 0:n1] for x in range(1, 8)]
-    seg = lambda b, x: b[:, n1 * x:n1 * x + n1]
-    e0 = ts(t[0], T.iz[:, 0:n1], 0.0, None, A.is_equal, None, [gz], n1)
-    e16 = ts(t[1], T.iz[:, 0:n1], -16.0, None, A.is_equal, None, [gz], n1)
-    r16 = ts(t[2], T.ir[:, 0:n1], 0.0, None, A.is_equal, None, [gr], n1)
-    u = ts(t[3], T.ip[:, 0:n1], -1.0, 15.0, A.mult, A.add, [gi], n1)
-    ur = tt(t[4], t[3], t[2], A.mult, [u, r16], 2 * n1)
-    base = tt(t[5], t[4], t[0], A.add, [ur, e0], 2 * n1)
-    rh = ts(t[6], t[2], -float(HALF), None, A.mult, None, [r16], n1)
-    s2 = ts(t[3], t[5], C_LO + C_HI, None, A.mult, None, [base], n1)
-    sel = [ts(seg(T.sel, 0), t[5], C_LO, None, A.mult, None, [base], n1), ts(seg(T.sel, 1), t[5], C_HI, None, A.mult, None, [base], n1),
-           tt(seg(T.sel, 2), t[3], t[6], A.add, [s2, rh], 2 * n1)]
-    selx = [tt(seg(T.selx, 0), t[0], t[1], A.subtract, [e0, e16], 2 * n1), cp(seg(T.selx, 1), t[1], [e16], n1),
-            ts(seg(T.selx, 2), t[1], 0.0, None, A.mult, None, [e16], n1)]
+    t = [T.tmp[:, n1 * x:n1 * x + n1] for x in range(12)]
+    e0 = ts(t[0], T.iz[:, 0:n1], 0.0, 16.0, A.is_equal, A.mult, [gz], n1)
+    r16 = ts(t[1], T.ir[:, 0:n1], 0.0, None, A.is_equal, None, [gr], n1)
+    ex = ts(t[2], T.iz[:, 0:n1], -32.0, None, A.is_equal, None, [gz], n1)
+    eh = ts(t[3], T.iz[:, 0:n1], -48.0, None, A.is_equal, None, [gz], n1)
+    u = ts(t[4], T.ip[:, 0:n1], -1.0, 15.0, A.mult, A.add, [gi], n1)
+    ur = tt(t[5], t[4], t[1], A.mult, [u, r16], 2 * n1)
+    base = tt(t[6], t[5], t[0], A.add, [ur, e0], 2 * n1)
+    lo = tt(t[7], t[2], t[3], A.subtract, [ex, eh], 2 * n1)
+    rh = ts(t[8], t[1], -float(HALF), None, A.mult, None, [r16], n1)
+    sel = []
+    for x, (c, more, made) in enumerate([(C_LO, t[7], lo), (C_HI, t[3], eh), (C_LO + C_HI, t[8], rh)]):
+        wt = ts(t[9 + x], t[6], c, None, A.mult, None, [base], n1)
+        sel.append(tt(T.sel[:, n1 * x:n1 * x + n1], t[9 + x], more, A.add, [wt, made], 2 * n1))
     e4 = [ts(T.e4[0:32, 144 * x:144 * x + 144], T.ie[0:32, 144 * x:144 * x + 144], 0.0, T.m4[0:32, x:x + 1], A.is_equal, A.mult, [ge, m4], 144) for x in range(4)]
-    PA = [T["ps%d" % (2 * h)] for h in range(NS)]
-    PK = [T["ps%d" % (2 * h + 1)] for h in range(NS)]
-    ones = [fill(PA[h][:, 0:128], 1.0 / 16, [], 128) for h in range(NS)]
+    PA, PT = [T["ps%d" % h] for h in range(NS)], [T["ps%d" % (NS + x)] for x in range(2)]
+    ones = [fill(PA[h][:, 0:128], 1.0, [], 128) for h in range(NS)]
 
     brh = [affine(e, T.brh[0:32, a:a + 384], T.brs[0:32, a:a + 384], [ldb, hb], 384, add=T.hb[0:32, 0:1]) for e, a in (("V", 0), ("S", 384))]
-    PB = PK[0]
+    PB = PT[0]
     bl = [mm([(PB[:, 48 * x:48 * x + 48], T.e4[0:32, 144 * x + 15 - b:144 * x + 143 - b], T.brh[0:32, b::16]) for b in range(16)],
              brh + [e4[x]], add=True) for x in range(4)]
     blo = ts(T.blo[:], PB[:, 0:192], float(HALF), None, A.add, None, bl, 192)
@@ -174,63 +172,57 @@ def build(g, core, T, topo):
     qbd = dma("Y", [(T.qblk[16 * x:16 * x + 16, x * N * Q + Q:(x + 1) * N * Q], T.qall[16 * x:16 * x + 16, Q:N * Q]) for x in range(8)],
               "qbd", 3 * 256 * Q, zero + [qarr])
 
-    ldk2 = dma("Y", [(T.kw[:, KA:S], T.k[:, KA:S])], "ldk2", 256 * (S - KA), [gg])
-    ldv = dma("Y", [(T.vw[:], T.v[:])], "ldv", 256 * S, [ldn, ldk, ldk2])
-    slot = [0]
-    def newlist(w):
-        slot[0] += 1
-        return lambda a=0, b=w, o=8 * (slot[0] - 1): T.lst[:, o + a:o + b]
-
-    cur = []
-    for h, (a0, w) in enumerate(SUBS):
-        L = newlist(w)
-        cur.append((L(), [cp(L(), T.ent[:, a0:a0 + w], [lde], 8)]))
-    last = [[] for _h in SUBS]
-    accin, lastrl = None, [None] * NS
+    ldk2 = dma("Y", [(T.kw[:, KA:S], T.k[:, KA:S])], "ldk2", 256 * (S - KA), [gg]) if KA < S else None
+    ldv = dma("Y", [(T.vw[:], T.v[:])], "ldv", 256 * S, [ldn, ldk, ldk2, gg])
+    lst = lambda k, a, b: T.lst[:, 8 * k + a:8 * k + b]
+    first = cp(lst(0, 0, 8), T.ent[:], [lde], 8)
+    cur = [(lst(0, W * h, W * h + W), [first]) for h in range(NS)]
+    last = [[] for _h in range(NS)]
+    accin, relus = None, [blo, None]
     for s in range(N):
-        terms = []
-        for h, (a0, w) in enumerate(SUBS):
-            n = 16 * w
+        for h in range(NS):
             L, rdy = cur[h]
             lead[0] = COST["lead"] * (NS - 1 - h)
-            c0, k0 = 64 * h, 1024 * h
-            cc, cf = T.cu[:, c0:c0 + n], T.ch[:, c0:c0 + n]
-            B, X = T.bs[0:32 * w, 128 * h:128 * h + 128], T.bx[0:32 * w, 128 * h:128 * h + 128]
-            K, rr = PK[h][:, 0:n3], T.rr[:, 192 * h:192 * h + n3]
+            c0 = n1 * h
+            cc, cf, B = T.cu[:, c0:c0 + n1], T.ch[:, c0:c0 + n1], T.bs[:, 128 * h:128 * h + 128]
+            K, rr = PA[h][:, 128:128 + n3], T.rr[:, n3 * h:n3 * h + n3]
             for step in range(2):
                 far = s > 0 and step == 0
                 win, have = (T.nb2 if far else T.nbw)[:, :].indirect(L), rdy + last[h] + (nb2 if far else [ldn])
-                cg = cp(cc, win, have, -n)
-                c16 = affine("S", cf, win, have + [hb], -n, add=T.hb[:, 0:1])
-                tu = [mm([(PK[h][32 * c:32 * c + 32, 256 + 16 * x:256 + 16 * x + 16], T.turn[:, 32 * x:32 * x + 32], T.ch[:, c0 + 16 * c:c0 + 16 * c + 16])
-                          for x in range(8)], [c16, turn, blo, lastrl[h]]) for c in range(w)]
-                ex = affine("VS", X, PK[h][0:32 * w, 256:384], tu + [xb], 128, add=T.xb[0:32 * w, 0:1])
-                px = mm([(K, X, T.selx[0:32 * w, 0:n3])], [ex] + selx, stop=False)
-                pe1, j0 = [], 0
-                for cnt in PIECES[w]:
-                    ga = affine("VS", T.kg[:, k0 + 16 * j0:k0 + 16 * (j0 + cnt)], T.kw[:, :].indirect(T.cu[:, c0 + j0:c0 + j0 + cnt]), [cg, ldk, ldk2], -16 * cnt)
-                    pe1.append(mm([(PA[h][32 * (j // 16):32 * (j // 16) + 16, (j % 16):128:16], T.kg[:, k0 + 16 * j:k0 + 16 * j + 16],
-                                    T.qblk[:, s * Q + 16 * a0 + j::N * Q]) for j in range(j0, j0 + cnt)], [ga, ones[h]] + (qb0 if s == 0 else [qbd])))
+                cg = cp(cc, win, have, -n1)
+                c16 = affine("S", cf, win, have + [hb], -n1, add=T.hb[:, 0:1])
+                tu = [mm([(PA[h][64 * c + 32:64 * c + 64, 16 * x:16 * x + 16], T.turn[:, 32 * x:32 * x + 32], T.ch[:, c0 + 16 * c:c0 + 16 * c + 16])
+                          for x in range(8)], [c16, turn, ones[h]]) for c in range(W)]
+                pe1, j0 = [], c0
+                for cnt in PIECES:
+                    ga = affine("VS", T.kg[:, 16 * j0:16 * (j0 + cnt)], T.kw[:, :].indirect(T.cu[:, j0:j0 + cnt]), [cg, ldk, ldk2], -16 * cnt)
+                    pe1.append(mm([(PA[h][64 * (j // 16 % W):64 * (j // 16 % W) + 16, (j % 16):128:16], T.kg[:, 16 * j:16 * j + 16],
+                                    T.qblk[:, s * Q + j::N * Q]) for j in range(j0, j0 + cnt)], [ga, ones[h]] + (qb0 if s == 0 else [qbd])))
                     j0 += cnt
-                ev = affine("VS", B, PA[h][0:32 * w, 0:128], pe1, 128, mul=16.0)
-                p2 = mm([(K, B, T.sel[0:32 * w, 0:n3])], [ev, px] + sel, start=False)
-                sc = vec(dur(n3), (lambda rr=rr, K=K: V.tensor_tensor_scan(rr, T.reset[:, 0:n3], K, 0.0, A.add, A.max)), [p2, reset])
-                Ln = newlist(w)
-                top = lambda x, c: T.rr[:, 192 * h + n1 * x + 16 * c + 15:192 * h + n1 * x + 16 * c + 16]
-                rdy = [ts(Ln(c, c + 1), top(1, c), top(2, c), top(0, c), A.subtract, A.add, [sc], 1) for c in range(w)]
-                L = Ln()
+                ev = affine("VS", B, PA[h][:, 0:128], pe1 + tu + [xb], 128, add=T.xb[:, 0:1])
+                p2 = mm([(K, B, T.sel[:])], [ev] + sel)
+                sc = vec(dur(n3), (lambda rr=rr, K=K: V.tensor_tensor_scan(rr, T.reset[:], K, 0.0, A.add, A.max)), [p2, reset])
+                k = 2 * s + step + 1
+                top = lambda x, c: T.rr[:, n3 * h + n1 * x + 16 * c + 15:n3 * h + n1 * x + 16 * c + 16]
+                rdy = [ts(lst(k, W * h + c, W * h + c + 1), top(1, c), top(2, c), top(0, c), A.subtract, A.add, [sc], 1) for c in range(W)]
+                L = lst(k, W * h, W * h + W)
                 last[h] = rdy
-            x0 = s * Q + 16 * a0
             if s < N - 1:
-                Li = T.lin[:, 8 * (s * NS + h):8 * (s * NS + h) + w]
+                Li = T.lin[:, 8 * (s * NS + h):8 * (s * NS + h) + W]
                 sem = "la%d_%d" % (s, h)
                 cur[h] = (Li, [send((lambda Li=Li, L=L, sem=sem: g.remote_dma(Li, L, T.sem[sem], T.sem.sent, pid, rid, mask)), rdy, sem, n_in, n_out, 1024)])
-            kq = tt(T.kq[:, x0:x0 + n], T.kw[:, :].indirect(L), qs(s, 16 * a0, 16 * a0 + n), A.mult, rdy + [ldq if s == 0 else qarr], -n)
-            ps, rs = PK[h][:, 384:384 + n], T.rs[:, x0:x0 + n]
-            sm = mm([(ps, T.bones[:], T.kq[:, x0:x0 + n])], [kq, bones])
-            lastrl[h] = op([("V", dur(n), lambda rs=rs, ps=ps: V.tensor_scalar(rs, ps, 0.0, None, A.max)),
-                            ("S", dur(n), lambda rs=rs, ps=ps: Sc.activation(rs, ps, F.Relu))], [sm])
-            terms.append(tt(T.term[:, x0:x0 + n], T.vw[:, :].indirect(L), rs, A.mult, [lastrl[h], ldv], -n))
+
+        terms = []
+        for x, hs in enumerate(TERMS if s < N - 1 else TAILS):
+            lead[0] = COST["lead"] * (NS - 1 - hs[-1])
+            a, n = n1 * hs[0], n1 * len(hs)
+            L, rdy = lst(2 * s + 2, W * hs[0], W * hs[-1] + W), [i for h in hs for i in last[h]]
+            kq, ps, rs = T.kq[:, s * Q + a:s * Q + a + n], PT[x % 2][:, 0:n], T.rs[:, s * Q + a:s * Q + a + n]
+            m = tt(kq, T.kw[:, :].indirect(L), qs(s, a, a + n), A.mult, rdy + [ldq if s == 0 else qarr], -n)
+            sm = mm([(ps, T.bones[:], kq)], [m, bones, relus[x % 2]])
+            relus[x % 2] = op([("V", dur(n), lambda rs=rs, ps=ps: V.tensor_scalar(rs, ps, 0.0, None, A.max)),
+                               ("S", dur(n), lambda rs=rs, ps=ps: Sc.activation(rs, ps, F.Relu))], [sm])
+            terms.append(tt(T.term[:, s * Q + a:s * Q + a + n], T.vw[:, :].indirect(L), rs, A.mult, [relus[x % 2], ldv], -n))
 
         def accsend(a, b, sem, s=s):
             dst, src = T.acc[:, s * Q + a:s * Q + b], T.term[:, s * Q + a:s * Q + b]
@@ -241,10 +233,10 @@ def build(g, core, T, topo):
         if s < N - 1:
             accin = send((lambda f=accsend, s=s: f(0, Q, "aa%d" % s)), terms + [accin], "aa%d" % s, n_in, n_out, 1024 * Q)
         else:
-            for h, (a0, w) in enumerate(SUBS):
-                a, b = 16 * a0, 16 * (a0 + w)
-                fa = send((lambda f=accsend, a=a, b=b, h=h: f(a, b, "fa%d" % h)), [terms[h], accin], "fa%d" % h, n_in, n_out, 16384 * w)
-                dma("Y", [(T.y[:, a:b], T.acc[:, s * Q + a:s * Q + b])], "st%d" % h, 8192 * w, [fa])
+            for x, hs in enumerate(TAILS):
+                a, b = n1 * hs[0], n1 * hs[-1] + n1
+                fa = send((lambda f=accsend, a=a, b=b, x=x: f(a, b, "fa%d" % x)), [terms[x], accin], "fa%d" % x, n_in, n_out, 1024 * (b - a))
+                dma("Y", [(T.y[:, a:b], T.acc[:, s * Q + a:s * Q + b])], "st%d" % x, 512 * (b - a), [fa])
     return ops, sent[0]
 
 

@@ -3,14 +3,17 @@ from concourse.mybir import AluOpType, ActivationFunctionType
 
 S, Q, N = 3072, 128, 4
 HALF = S // 2
-NS, W = 4, 2
-PIECES = [18, 14]
+SUBS = [2, 2, 2, 2]
+NS, COL = len(SUBS), [sum(SUBS[:h]) for h in range(len(SUBS))]
+LEAD = [1.5, 1.0, 0.5, 0.0]
+PIECES = {2: [18, 14], 1: [16]}
+SENDS = [[0, 1], [2], [3]]
 TERMS = [[0, 1, 2, 3]]
-TAILS = [[0, 1], [2, 3]]
+TAILS = [[0, 1, 2], [3]]
 KA = 3072
 NB2 = 16
 C_LO, C_HI = 64.0, 3200.0
-COST = dict(cycle=0.00088, gather=1.4, pe=0.00046, wait=0.25, dma=1.0, rate=4e5, issue=0.3, first=2.0, remote=1.2, look=0.5, margin=0.2, spare=0.1, lead=0.4)
+COST = dict(cycle=0.00083, gather=1.5, pe=0.00042, wait=0.28, dma=1.0, rate=4e5, issue=0.3, first=2.0, remote=1.2, look=0.5, margin=0.3, spare=0.1)
 
 SCRATCH = {
     "nbw": ("sbuf", [128, S], "int32"), "kw": ("sbuf", [128, S], "bfloat16"), "vw": ("sbuf", [128, S], "bfloat16"),
@@ -18,23 +21,23 @@ SCRATCH = {
     "brs": ("sbuf", [128, 768], "int32"), "brh": ("sbuf", [128, 768], "float16"),
     "qall": ("sbuf", [128, N * Q], "bfloat16"), "qblk": ("sbuf", [128, 8 * N * Q], "bfloat16"),
     "ent": ("sbuf", [128, 8], "int32"),
-    "lst": ("sbuf", [128, 8 * 9], "uint16"), "lin": ("sbuf", [128, 8 * 3 * NS], "uint16"),
+    "lst": ("sbuf", [128, 16 * 9], "uint16"), "lin": ("sbuf", [128, 8 * 3 * NS], "uint16"),
     "cu": ("sbuf", [128, Q], "uint16"), "ch": ("sbuf", [128, Q], "float16"),
     "kg": ("sbuf", [128, 16 * Q], "bfloat16"), "bs": ("sbuf", [128, 128 * NS], "float16"),
-    "rr": ("sbuf", [128, 96 * NS], "float32"),
-    "kq": ("sbuf", [128, N * Q], "bfloat16"), "rs": ("sbuf", [128, N * Q], "float32"),
+    "rr": ("sbuf", [128, 4 * Q], "float32"),
+    "kq": ("sbuf", [128, N * Q], "float16"), "rs": ("sbuf", [128, N * Q], "float32"),
     "term": ("sbuf", [128, N * Q], "float32"), "acc": ("sbuf", [128, N * Q], "float32"),
     "pi": ("sbuf", [128, 4], "int32"), "pb": ("sbuf", [128, 4], "int32"), "pf": ("sbuf", [128, 4], "float32"),
-    "i8": ("sbuf", [128, 8], "float32"), "ig": ("sbuf", [128, 128], "float32"), "it": ("sbuf", [128, 256], "float32"),
-    "ip": ("sbuf", [128, 192], "float32"), "iz": ("sbuf", [128, 64], "float32"), "ir": ("sbuf", [128, 64], "float32"),
-    "ie": ("sbuf", [128, 576], "float32"), "m4": ("sbuf", [128, 4], "float32"), "hb": ("sbuf", [128, 4], "float32"), "xb": ("sbuf", [128, 4], "float32"),
-    "gm8": ("sbuf", [128, 8], "float32"), "bones": ("sbuf", [128, 128], "bfloat16"), "turn": ("sbuf", [128, 256], "float16"),
-    "reset": ("sbuf", [128, 96], "float32"), "sel": ("sbuf", [128, 96], "float16"),
-    "tmp": ("sbuf", [128, 32 * 12], "float32"), "e4": ("sbuf", [128, 576], "float16"),
+    "ig": ("sbuf", [128, 128], "float32"), "it": ("sbuf", [128, 256], "float32"), "ip": ("sbuf", [128, 128], "float32"),
+    "ie": ("sbuf", [128, 576], "float32"), "hb": ("sbuf", [128, 4], "float32"), "xb": ("sbuf", [128, 4], "float32"),
+    "gm8": ("sbuf", [128, 8], "float32"), "bones": ("sbuf", [128, 128], "float16"), "turn": ("sbuf", [128, 256], "float16"),
+    "reset": ("sbuf", [128, 128], "float32"), "sel": ("sbuf", [128, 64], "float16"), "sel48": ("sbuf", [128, 96], "float16"),
+    "sel64": ("sbuf", [128, 128], "float16"), "diag": ("sbuf", [128, 16], "float32"),
+    "tmp": ("sbuf", [128, 16 * 9], "float32"), "e4": ("sbuf", [128, 576], "float16"),
 }
-for _b in range(NS + 2):
+for _b in range(min(8, NS + 2)):
     SCRATCH["ps%d" % _b] = ("psum", [128, 512], "float32")
-SEMAPHORES = (["cV", "cS", "cP", "cG", "ldq", "ldb", "lde", "ldn", "ldk", "ldk2", "ldv", "sent", "qarr", "bla", "qbd"]
+SEMAPHORES = (["cV", "cS", "cP", "cG", "ldq", "ldbY", "ldbS", "lde", "ldn", "ldk", "ldk2", "ldv", "sent", "qarr", "qar1", "bla", "qbd"]
               + ["la%d_%d" % (s, h) for s in range(3) for h in range(NS)]
               + ["aa%d" % s for s in range(3)] + ["fa%d" % h for h in range(len(TAILS))] + ["st%d" % h for h in range(len(TAILS))])
 
@@ -53,7 +56,7 @@ def build(g, core, T, topo):
     gdur = lambda n, q: (0.05 if q == "V" else 0.065) + COST["gather"] * n * cy
 
     def op(forms, needs, sig=None, kind="c", nbytes=0):
-        ops.append(dict(forms=forms, needs=sorted(set(x for x in needs if x is not None)), sig=sig, kind=kind, bytes=nbytes, after=[], boost=lead[0]))
+        ops.append(dict(forms=forms, needs=sorted(set(x for x in needs if x is not None)), sig=sig, kind=kind, bytes=nbytes, after=[], queued=[], boost=lead[0]))
         return len(ops) - 1
     def vec(d, emit, needs):
         return op([("V", d, emit)], needs)
@@ -95,13 +98,13 @@ def build(g, core, T, topo):
         return op([], [a], sig=(sem, cnt), kind="a")
 
     qs = lambda s, a=0, b=Q: T.qall[:, s * Q + a:s * Q + b]
-    ldb = dma("S", [(T.brs[0:32, :], T.br[:])], "ldb", 4 * 8 * S)
+    ldb = [dma(e, [(T.brs[8 * x:8 * x + 8, :], T.br[:, 768 * x:768 * x + 768]) for x in (y, y + 1)], "ldb" + e, 2 * 8 * S) for e, y in (("Y", 0), ("S", 2))]
     ldq = dma("Y", [(qs(0), T.q[:])], "ldq", 256 * Q)
     lde = dma("S", [(T.ent[:], T.entry[:])], "lde", 4096)
     ldn = dma("Y", [(T.nbw[:], T.nb[:])], "ldn", 512 * S)
-    ldk = dma("S", [(T.kw[:, 0:KA], T.k[:, 0:KA])], "ldk", 256 * KA) if KA else None
-    ops[ldn]["after"], ops[lde]["after"] = [ldb, ldq, lde], [ldb]
-    if KA: ops[ldk]["after"] = [ldn]
+    ldk = dma("Y", [(T.kw[:, 0:KA], T.k[:, 0:KA])], "ldk", 256 * KA)
+    ops[ldn]["after"], ops[lde]["after"], ops[ldq]["after"] = [ldq, lde], ldb, ldb
+    ops[ldk]["after"] = ops[ldk]["queued"] = [ldn]
 
     others = [c for c in T.cores if c != core]
     def qmask(c):
@@ -110,59 +113,62 @@ def build(g, core, T, topo):
             if d != c: m &= topo.mask(c, d)
         return m
     bits = lambda m: bin(m).count("1")
-    def qsend():
-        ids = [DstId(rid=topo.addr(d)[0], pnc=topo.addr(d)[1]) for d in others]
-        dsts = [qs((T.rank_of(d) - rank) % N) for d in others]
-        tr = RemoteDMATransfer(dst_ids=ids, dma_engine_mask=qmask(core), remote_sem=T.sem.qarr, srcs=[qs(0)], dsts=dsts)
+    def qsend(to, sem):
+        ids = [DstId(rid=topo.addr(d)[0], pnc=topo.addr(d)[1]) for d in to]
+        dsts = [qs((T.rank_of(d) - rank) % N) for d in to]
+        tr = RemoteDMATransfer(dst_ids=ids, dma_engine_mask=qmask(core), remote_sem=T.sem[sem], srcs=[qs(0)], dsts=dsts)
         return g.remote_dma_fused([tr], local_sem=T.sem.sent)
 
-    n3 = 48 * W
     gp = op([("G", 0.13, lambda: g.iota(T.pi[:, 0:1], [[0, 1]], 0, 1))], [])
-    g8 = iota(T.i8[:], [[1, 8]], 0, 8)
-    ge = iota(T.ie[0:32, :], [[4, 4], [1, 144]], -4, 576, -15)
-    gi = iota(T.ip[:, 0:n3], [[0, 3 * W], [1, 16]], 0, n3)
-    gz = iota(T.iz[:, 0:16 * W], [[64, W], [1, 16]], -1, 16 * W)
-    gr = iota(T.ir[:, 0:16 * W], [[64, W], [0, 16]], -1, 16 * W, 16)
+    ge = iota(T.ie[0:32, :], [[128, 4], [1, 144]], -16, 576, -15)
+    gi = iota(T.ip[:], [[0, 8], [1, 16]], 0, 128)
     gt = iota(T.it[:], [[16, 8], [0, 2], [1, 16]], -1, 256)
-    qarr = send(qsend, [ldq], "qarr", sum(bits(qmask(c)) for c in others), bits(qmask(core)), 3 * 256 * Q)
-    b0 = ts(T.pb[:, 0:1], T.pi[:, 0:1], 3, None, A.bitwise_and, None, [gp], 1)
-    b1 = ts(T.pb[:, 1:2], T.pi[:, 0:1], 48, None, A.bitwise_and, None, [gp], 1)
-    b2 = ts(T.pb[:, 2:3], T.pi[:, 0:1], 4, None, A.arith_shift_right, None, [gp], 1)
-    pf = cp(T.pf[:, 0:3], T.pb[:, 0:3], [b0, b1, b2], 3)
-    p3, p48, pg = T.pf[:, 0:1], T.pf[:, 1:2], T.pf[:, 2:3]
+    qar1 = send(lambda: qsend([nxt], "qar1"), [ldq], "qar1", bits(qmask(prv)), bits(qmask(core)), 256 * Q)
+    b1 = ts(T.pb[:, 0:1], T.pi[:, 0:1], 63, None, A.bitwise_and, None, [gp], 1)
+    b2 = ts(T.pb[:, 1:2], T.pi[:, 0:1], 4, None, A.arith_shift_right, None, [gp], 1)
+    b3 = ts(T.pb[:, 2:3], T.pi[:, 0:1], 15, None, A.bitwise_and, None, [gp], 1)
+    pf = cp(T.pf[:, 0:3], T.pb[:, 0:3], [b1, b2, b3], 3)
+    row, pg, ip = T.pf[:, 0:1], T.pf[:, 1:2], T.ip[:, 0:16]
     hb = fill(T.hb[:], -float(HALF), [], 4)
-    xb = ts(T.xb[:, 0:1], p48, 48.0, 32768.0 + HALF, A.is_equal, A.mult, [pf], 1)
-    gm8 = ts(T.gm8[:], T.i8[:], pg, None, A.is_equal, None, [pf, g8], 8)
-    m4 = ts(T.m4[:], T.i8[:, 0:4], p3, None, A.is_equal, None, [pf, g8], 4)
+    xb = ts(T.xb[:, 0:1], row, 48.0, 32768.0 + HALF, A.is_ge, A.mult, [pf], 1)
+    r16 = ts(T.xb[:, 1:2], row, 16.0, None, A.is_equal, None, [pf], 1)
+    rh = ts(T.xb[:, 2:3], row, 16.0, -float(HALF), A.is_equal, A.mult, [pf], 1)
+    gm8 = ts(T.gm8[:], T.ip[:, 0:8], pg, None, A.is_equal, None, [pf, gi], 8)
     turn = ts(T.turn[:], T.it[:], 0.0, None, A.is_equal, None, [gt], 256)
-    reset = ts(T.reset[:, 0:n3], T.ip[:, 0:n3], 0.0, -1e9, A.is_equal, A.mult, [gi], n3)
-    n1 = 16 * W
-    t = [T.tmp[:, n1 * x:n1 * x + n1] for x in range(12)]
-    e0 = ts(t[0], T.iz[:, 0:n1], 0.0, 16.0, A.is_equal, A.mult, [gz], n1)
-    r16 = ts(t[1], T.ir[:, 0:n1], 0.0, None, A.is_equal, None, [gr], n1)
-    ex = ts(t[2], T.iz[:, 0:n1], -32.0, None, A.is_equal, None, [gz], n1)
-    eh = ts(t[3], T.iz[:, 0:n1], -48.0, None, A.is_equal, None, [gz], n1)
-    u = ts(t[4], T.ip[:, 0:n1], -1.0, 15.0, A.mult, A.add, [gi], n1)
-    ur = tt(t[5], t[4], t[1], A.mult, [u, r16], 2 * n1)
-    base = tt(t[6], t[5], t[0], A.add, [ur, e0], 2 * n1)
-    lo = tt(t[7], t[2], t[3], A.subtract, [ex, eh], 2 * n1)
-    rh = ts(t[8], t[1], -float(HALF), None, A.mult, None, [r16], n1)
-    sel = []
-    for x, (c, more, made) in enumerate([(C_LO, t[7], lo), (C_HI, t[3], eh), (C_LO + C_HI, t[8], rh)]):
-        wt = ts(t[9 + x], t[6], c, None, A.mult, None, [base], n1)
-        sel.append(tt(T.sel[:, n1 * x:n1 * x + n1], t[9 + x], more, A.add, [wt, made], 2 * n1))
-    e4 = [ts(T.e4[0:32, 144 * x:144 * x + 144], T.ie[0:32, 144 * x:144 * x + 144], 0.0, T.m4[0:32, x:x + 1], A.is_equal, A.mult, [ge, m4], 144) for x in range(4)]
-    PA, PT = [T["ps%d" % h] for h in range(NS)], [T["ps%d" % (NS + x)] for x in range(2)]
+    reset = ts(T.reset[:], T.ip[:], 0.0, -1e9, A.is_equal, A.mult, [gi], 128)
+    t = [T.tmp[:, 16 * x:16 * x + 16] for x in range(9)]
+    e0 = ts(t[0], ip, row, 16.0, A.is_equal, A.mult, [gi, pf], 16)
+    ex = ts(t[1], ip, 32.0, row, A.add, A.is_equal, [gi, pf], 16)
+    eh = ts(t[2], ip, 48.0, row, A.add, A.is_equal, [gi, pf], 16)
+    u = ts(t[3], ip, -1.0, 15.0, A.mult, A.add, [gi], 16)
+    ur = ts(t[4], t[3], T.xb[:, 1:2], None, A.mult, None, [u, r16], 16)
+    base = tt(t[5], t[4], t[0], A.add, [ur, e0], 32)
+    lo = tt(t[6], t[1], t[2], A.subtract, [ex, eh], 32)
+    diag = ts(T.diag[:], ip, T.pf[:, 2:3], None, A.is_equal, None, [gi, pf], 16)
+    sel = [ts(T.sel[:, 32:48], t[5], C_LO + C_HI, T.xb[:, 2:3], A.mult, A.add, [base, rh], 16),
+           ts(T.sel[:, 48:64], ip, row, None, A.is_equal, None, [gi, pf], 16)]
+    for x, (c, more, made) in enumerate([(C_LO, t[6], lo), (C_HI, t[2], eh)]):
+        wt = ts(t[7 + x], t[5], c, None, A.mult, None, [base], 16)
+        sel.append(tt(T.sel[:, 16 * x:16 * x + 16], t[7 + x], more, A.add, [wt, made], 32))
+    blk = [ts(T.hb[:, 1 + c:2 + c], pg, 4.0, None, [A.is_lt, A.is_ge][c], None, [pf, hb], 1) for c in range(2)]
+    sels = {m: [ts(T["sel%d" % m][:, m * c:m * c + m], T.sel[:, 0:m], T.hb[:, 1 + c:2 + c], None, A.mult, None, sel + [blk[c]], m) for c in range(2)]
+            for m in (48, 64)}
+    e4 = [ts(T.e4[0:32, 144 * x:144 * x + 144], T.ie[0:32, 144 * x:144 * x + 144], 0.0, None, A.is_equal, None, [ge], 144) for x in range(4)]
+    PA, PT = [T["ps%d" % h] for h in range(NS)], [T["ps%d" % min(NS + x, 7)] for x in range(2)]
     ones = [fill(PA[h][:, 0:128], 1.0, [], 128) for h in range(NS)]
 
-    brh = [affine(e, T.brh[0:32, a:a + 384], T.brs[0:32, a:a + 384], [ldb, hb], 384, add=T.hb[0:32, 0:1]) for e, a in (("V", 0), ("S", 384))]
+    brh = [affine(e, T.brh[0:32, a:a + 384], T.brs[0:32, a:a + 384], ldb + [hb], 384, add=T.hb[0:32, 0:1]) for e, a in (("V", 0), ("S", 384))]
     PB = PT[0]
     bl = [mm([(PB[:, 48 * x:48 * x + 48], T.e4[0:32, 144 * x + 15 - b:144 * x + 143 - b], T.brh[0:32, b::16]) for b in range(16)],
              brh + [e4[x]], add=True) for x in range(4)]
     blo = ts(T.blo[:], PB[:, 0:192], float(HALF), None, A.add, None, bl, 192)
-    bla = send(lambda: g.remote_dma(T.bli[:], T.blo[:], T.sem.bla, T.sem.sent, pid, rid, mask), [blo, qarr - 1], "bla", n_in, n_out, 384 * 128)
+    bla = send(lambda: g.remote_dma(T.bli[:], T.blo[:], T.sem.bla, T.sem.sent, pid, rid, mask), [blo, qar1 - 1], "bla", n_in, n_out, 384 * 128)
     gg = iota(T.ig[:], [[1, 8], [0, 16]], 0, 128)
     ops[gg]["after"] = [bla - 1]
+    ops[qar1 - 1]["forms"] = [("G", COST["issue"] + COST["first"], ops[qar1 - 1]["forms"][0][2])]
+    qarr = send(lambda: qsend([c for c in others if c != nxt], "qarr"), [ldq], "qarr", sum(bits(qmask(c)) for c in others if c != prv), bits(qmask(core)), 2 * 256 * Q)
+    ops[qarr - 1]["after"] = [bla - 1]
+    for i in [ge, hb, blo, bla - 1, qar1 - 1, ldq] + e4 + brh + bl + ldb: ops[i]["boost"] = 8.0
     bones = ts(T.bones[:], T.ig[:], pg, None, A.is_equal, None, [pf, gg], 128)
     z = 192 // NB2
     nb2 = [affine("VS", T.nb2[:, 16 * z * x:16 * z * (x + 1)], T.nbw[:, :].indirect(T.bli[:, z * x:z * (x + 1)]), [bla, ldn], -16 * z) for x in range(NB2)]
@@ -170,22 +176,22 @@ def build(g, core, T, topo):
     qb0 = [affine("VS", T.qblk[:, x * N * Q:x * N * Q + Q], qs(0), [gm8, ldq], 64, mul=T.gm8[:, x:x + 1]) for x in range(8)]
     zero = [fill(T.qblk[:, x * N * Q + Q:(x + 1) * N * Q], 0.0, [], 192) for x in range(8)]
     qbd = dma("Y", [(T.qblk[16 * x:16 * x + 16, x * N * Q + Q:(x + 1) * N * Q], T.qall[16 * x:16 * x + 16, Q:N * Q]) for x in range(8)],
-              "qbd", 3 * 256 * Q, zero + [qarr])
+              "qbd", 3 * 256 * Q, zero + [qarr, qar1])
 
     ldk2 = dma("Y", [(T.kw[:, KA:S], T.k[:, KA:S])], "ldk2", 256 * (S - KA), [gg]) if KA < S else None
     ldv = dma("Y", [(T.vw[:], T.v[:])], "ldv", 256 * S, [ldn, ldk, ldk2, gg])
-    lst = lambda k, a, b: T.lst[:, 8 * k + a:8 * k + b]
-    first = cp(lst(0, 0, 8), T.ent[:], [lde], 8)
-    cur = [(lst(0, W * h, W * h + W), [first]) for h in range(NS)]
+    def lst(k, h, a, b):
+        o = 16 * k + (2 * h if k % 2 or k == 0 else COL[h])
+        return T.lst[:, o + a:o + b]
+    cur = [(lst(0, h, 0, w), [cp(lst(0, h, 0, w), T.ent[:, COL[h]:COL[h] + w], [lde], 8)]) for h, w in enumerate(SUBS)]
     last = [[] for _h in range(NS)]
-    accin, relus = None, [blo, None]
+    accin, relus = None, {PT[0].name: blo}
     for s in range(N):
-        for h in range(NS):
+        for h, W in enumerate(SUBS):
             L, rdy = cur[h]
-            lead[0] = COST["lead"] * (NS - 1 - h)
-            c0 = n1 * h
-            cc, cf, B = T.cu[:, c0:c0 + n1], T.ch[:, c0:c0 + n1], T.bs[:, 128 * h:128 * h + 128]
-            K, rr = PA[h][:, 128:128 + n3], T.rr[:, n3 * h:n3 * h + n3]
+            lead[0] = LEAD[h]
+            c0, n1 = 16 * COL[h], 16 * W
+            cc, cf, B = T.cu[:, c0:c0 + n1], T.ch[:, c0:c0 + n1], T.bs[0:64 * W, 128 * h:128 * h + 128]
             for step in range(2):
                 far = s > 0 and step == 0
                 win, have = (T.nb2 if far else T.nbw)[:, :].indirect(L), rdy + last[h] + (nb2 if far else [ldn])
@@ -194,35 +200,49 @@ def build(g, core, T, topo):
                 tu = [mm([(PA[h][64 * c + 32:64 * c + 64, 16 * x:16 * x + 16], T.turn[:, 32 * x:32 * x + 32], T.ch[:, c0 + 16 * c:c0 + 16 * c + 16])
                           for x in range(8)], [c16, turn, ones[h]]) for c in range(W)]
                 pe1, j0 = [], c0
-                for cnt in PIECES:
+                for cnt in PIECES[W]:
                     ga = affine("VS", T.kg[:, 16 * j0:16 * (j0 + cnt)], T.kw[:, :].indirect(T.cu[:, j0:j0 + cnt]), [cg, ldk, ldk2], -16 * cnt)
-                    pe1.append(mm([(PA[h][64 * (j // 16 % W):64 * (j // 16 % W) + 16, (j % 16):128:16], T.kg[:, 16 * j:16 * j + 16],
+                    pe1.append(mm([(PA[h][64 * ((j - c0) // 16):64 * ((j - c0) // 16) + 16, (j % 16):128:16], T.kg[:, 16 * j:16 * j + 16],
                                     T.qblk[:, s * Q + j::N * Q]) for j in range(j0, j0 + cnt)], [ga, ones[h]] + (qb0 if s == 0 else [qbd])))
                     j0 += cnt
-                ev = affine("VS", B, PA[h][:, 0:128], pe1 + tu + [xb], 128, add=T.xb[:, 0:1])
-                p2 = mm([(K, B, T.sel[:])], [ev] + sel)
-                sc = vec(dur(n3), (lambda rr=rr, K=K: V.tensor_tensor_scan(rr, T.reset[:], K, 0.0, A.add, A.max)), [p2, reset])
+                ev = affine("VS", B, PA[h][0:64 * W, 0:128], pe1 + tu + [xb], 128, add=T.xb[0:64 * W, 0:1])
                 k = 2 * s + step + 1
-                top = lambda x, c: T.rr[:, n3 * h + n1 * x + 16 * c + 15:n3 * h + n1 * x + 16 * c + 16]
-                rdy = [ts(lst(k, W * h + c, W * h + c + 1), top(1, c), top(2, c), top(0, c), A.subtract, A.add, [sc], 1) for c in range(W)]
-                L = lst(k, W * h, W * h + W)
+                m = 64 if k == 2 * N else 48
+                K, rr = PA[h][:, 128:128 + m * W], T.rr[:, 4 * c0:4 * c0 + m * W]
+                p2 = mm([(K, B, T["sel%d" % m][0:64 * W, 0:m * W])], [ev] + sels[m])
+                sc = vec(dur(m * W), (lambda rr=rr, K=K, n=m * W: V.tensor_tensor_scan(rr, T.reset[:, 0:n], K, 0.0, A.add, A.max)), [p2, reset])
+                top = lambda x, c: T.rr[:, 4 * c0 + m * c + 16 * x + 15:4 * c0 + m * c + 16 * x + 16]
+                rdy = [ts(lst(k, h, c, c + 1), top(1, c), top(2, c), top(0, c), A.subtract, A.add, [sc], 1) for c in range(W)]
+                L = lst(k, h, 0, W)
                 last[h] = rdy
-            if s < N - 1:
-                Li = T.lin[:, 8 * (s * NS + h):8 * (s * NS + h) + W]
-                sem = "la%d_%d" % (s, h)
-                cur[h] = (Li, [send((lambda Li=Li, L=L, sem=sem: g.remote_dma(Li, L, T.sem[sem], T.sem.sent, pid, rid, mask)), rdy, sem, n_in, n_out, 1024)])
+            if s == N - 1:
+                xs = [op([("V", dur(16), lambda o=T.kq[:, s * Q + c0 + 16 * c:s * Q + c0 + 16 * c + 16], a=top(3, c): V.tensor_scalar(o, T.diag[:], a, 0.0, A.mult, A.max)),
+                          ("S", dur(16), lambda o=T.kq[:, s * Q + c0 + 16 * c:s * Q + c0 + 16 * c + 16], a=top(3, c): Sc.activation(o, T.diag[:], F.Relu, scale=a))],
+                         [sc, diag]) for c in range(W)]
+                ps, vg = PA[h][:, 256:256 + n1], T.rs[:, s * Q + c0:s * Q + c0 + n1]
+                sm = mm([(ps, T.bones[:], T.kq[:, s * Q + c0:s * Q + c0 + n1])], xs + [bones])
+                val = affine("VS", vg, T.vw[:, :].indirect(L), rdy + [ldv], -n1)
+                last[h] = [tt(T.term[:, s * Q + c0:s * Q + c0 + n1], vg, ps, A.mult, [sm, val], n1)]
+            elif h in [x[-1] for x in SENDS]:
+                hs = [x for x in SENDS if x[-1] == h][0]
+                o, w = 8 * (s * NS + h), sum(SUBS[x] for x in hs)
+                Li, L, sem = T.lin[:, o:o + w], lst(k, hs[0], 0, w), "la%d_%d" % (s, h)
+                came = send((lambda Li=Li, L=L, sem=sem: g.remote_dma(Li, L, T.sem[sem], T.sem.sent, pid, rid, mask)), [i for x in hs for i in last[x]], sem, n_in, n_out, 1024)
+                for x in hs:
+                    cur[x] = (T.lin[:, o + COL[x] - COL[hs[0]]:o + COL[x] - COL[hs[0]] + SUBS[x]], [came])
 
         terms = []
-        for x, hs in enumerate(TERMS if s < N - 1 else TAILS):
-            lead[0] = COST["lead"] * (NS - 1 - hs[-1])
-            a, n = n1 * hs[0], n1 * len(hs)
-            L, rdy = lst(2 * s + 2, W * hs[0], W * hs[-1] + W), [i for h in hs for i in last[h]]
-            kq, ps, rs = T.kq[:, s * Q + a:s * Q + a + n], PT[x % 2][:, 0:n], T.rs[:, s * Q + a:s * Q + a + n]
-            m = tt(kq, T.kw[:, :].indirect(L), qs(s, a, a + n), A.mult, rdy + [ldq if s == 0 else qarr], -n)
-            sm = mm([(ps, T.bones[:], kq)], [m, bones, relus[x % 2]])
-            relus[x % 2] = op([("V", dur(n), lambda rs=rs, ps=ps: V.tensor_scalar(rs, ps, 0.0, None, A.max)),
-                               ("S", dur(n), lambda rs=rs, ps=ps: Sc.activation(rs, ps, F.Relu))], [sm])
-            terms.append(tt(T.term[:, s * Q + a:s * Q + a + n], T.vw[:, :].indirect(L), rs, A.mult, [relus[x % 2], ldv], -n))
+        for x, hs in enumerate(TERMS if s < N - 1 else []):
+            lead[0] = LEAD[hs[-1]]
+            a, n = 16 * COL[hs[0]], 16 * sum(SUBS[h] for h in hs)
+            L, rdy = lst(2 * s + 2, hs[0], 0, n // 16), [i for h in hs for i in last[h]]
+            bank = PT[x % 2]
+            kq, ps, rs = T.kq[:, s * Q + a:s * Q + a + n], bank[:, 0:n], T.rs[:, s * Q + a:s * Q + a + n]
+            m = tt(kq, T.kw[:, :].indirect(L), qs(s, a, a + n), A.mult, rdy + [ldq, qar1, qarr, qarr][s:s + 1], -n)
+            sm = mm([(ps, T.bones[:], kq)], [m, bones, relus.get(bank.name)])
+            relus[bank.name] = op([("V", dur(n), lambda rs=rs, ps=ps: V.tensor_scalar(rs, ps, 0.0, None, A.max)),
+                                   ("S", dur(n), lambda rs=rs, ps=ps: Sc.activation(rs, ps, F.Relu))], [sm])
+            terms.append(tt(T.term[:, s * Q + a:s * Q + a + n], T.vw[:, :].indirect(L), rs, A.mult, [relus[bank.name], ldv], -n))
 
         def accsend(a, b, sem, s=s):
             dst, src = T.acc[:, s * Q + a:s * Q + b], T.term[:, s * Q + a:s * Q + b]
@@ -234,8 +254,8 @@ def build(g, core, T, topo):
             accin = send((lambda f=accsend, s=s: f(0, Q, "aa%d" % s)), terms + [accin], "aa%d" % s, n_in, n_out, 1024 * Q)
         else:
             for x, hs in enumerate(TAILS):
-                a, b = n1 * hs[0], n1 * hs[-1] + n1
-                fa = send((lambda f=accsend, a=a, b=b, x=x: f(a, b, "fa%d" % x)), [terms[x], accin], "fa%d" % x, n_in, n_out, 1024 * (b - a))
+                a, b = 16 * COL[hs[0]], 16 * (COL[hs[-1]] + SUBS[hs[-1]])
+                fa = send((lambda f=accsend, a=a, b=b, x=x: f(a, b, "fa%d" % x)), [last[h][0] for h in hs] + [accin], "fa%d" % x, n_in, n_out, 1024 * (b - a))
                 dma("Y", [(T.y[:, a:b], T.acc[:, s * Q + a:s * Q + b])], "st%d" % x, 512 * (b - a), [fa])
     return ops, sent[0]
 
@@ -273,7 +293,6 @@ def schedule(ops):
         if x is None:
             done[i] = done[o["needs"][0]]
         else:
-            if o["kind"] == "r": d, first[0] = d + first[0], 0.0
             free[q] = t + d
             done[i] = t + d + wait
             if o["kind"] in "dr":

from concourse.bass import DstId, RemoteDMATransfer
from concourse.mybir import AluOpType, ActivationFunctionType

S, Q, N = 3072, 128, 4
HALF = S // 2
SUBS = [2, 2, 2, 2]
NS, COL = len(SUBS), [sum(SUBS[:h]) for h in range(len(SUBS))]
LEAD = [1.5, 1.0, 0.5, 0.0]
PIECES = {2: [18, 14], 1: [16]}
SENDS = [[0, 1], [2], [3]]
TERMS = [[0, 1, 2, 3]]
TAILS = [[0, 1, 2], [3]]
KA = 3072
NB2 = 16
C_LO, C_HI = 64.0, 3200.0
COST = dict(cycle=0.00083, gather=1.5, pe=0.00042, wait=0.28, dma=1.0, rate=4e5, issue=0.3, first=2.0, remote=1.2, look=0.5, margin=0.3, spare=0.1)

SCRATCH = {
    "nbw": ("sbuf", [128, S], "int32"), "kw": ("sbuf", [128, S], "bfloat16"), "vw": ("sbuf", [128, S], "bfloat16"),
    "nb2": ("sbuf", [128, S], "float32"), "blo": ("sbuf", [128, 192], "uint16"), "bli": ("sbuf", [128, 192], "uint16"),
    "brs": ("sbuf", [128, 768], "int32"), "brh": ("sbuf", [128, 768], "float16"),
    "qall": ("sbuf", [128, N * Q], "bfloat16"), "qblk": ("sbuf", [128, 8 * N * Q], "bfloat16"),
    "ent": ("sbuf", [128, 8], "int32"),
    "lst": ("sbuf", [128, 16 * 9], "uint16"), "lin": ("sbuf", [128, 8 * 3 * NS], "uint16"),
    "cu": ("sbuf", [128, Q], "uint16"), "ch": ("sbuf", [128, Q], "float16"),
    "kg": ("sbuf", [128, 16 * Q], "bfloat16"), "bs": ("sbuf", [128, 128 * NS], "float16"),
    "rr": ("sbuf", [128, 4 * Q], "float32"),
    "kq": ("sbuf", [128, N * Q], "float16"), "rs": ("sbuf", [128, N * Q], "float32"),
    "term": ("sbuf", [128, N * Q], "float32"), "acc": ("sbuf", [128, N * Q], "float32"),
    "pi": ("sbuf", [128, 4], "int32"), "pb": ("sbuf", [128, 4], "int32"), "pf": ("sbuf", [128, 4], "float32"),
    "ig": ("sbuf", [128, 128], "float32"), "it": ("sbuf", [128, 256], "float32"), "ip": ("sbuf", [128, 128], "float32"),
    "ie": ("sbuf", [128, 576], "float32"), "hb": ("sbuf", [128, 4], "float32"), "xb": ("sbuf", [128, 4], "float32"),
    "gm8": ("sbuf", [128, 8], "float32"), "bones": ("sbuf", [128, 128], "float16"), "turn": ("sbuf", [128, 256], "float16"),
    "reset": ("sbuf", [128, 128], "float32"), "sel": ("sbuf", [128, 64], "float16"), "sel48": ("sbuf", [128, 96], "float16"),
    "sel64": ("sbuf", [128, 128], "float16"), "diag": ("sbuf", [128, 16], "float32"),
    "tmp": ("sbuf", [128, 16 * 9], "float32"), "e4": ("sbuf", [128, 576], "float16"),
}
for _b in range(min(8, NS + 2)):
    SCRATCH["ps%d" % _b] = ("psum", [128, 512], "float32")
SEMAPHORES = (["cV", "cS", "cP", "cG", "ldq", "ldbY", "ldbS", "lde", "ldn", "ldk", "ldk2", "ldv", "sent", "qarr", "qar1", "bla", "qbd"]
              + ["la%d_%d" % (s, h) for s in range(3) for h in range(NS)]
              + ["aa%d" % s for s in range(3)] + ["fa%d" % h for h in range(len(TAILS))] + ["st%d" % h for h in range(len(TAILS))])


def build(g, core, T, topo):
    A, F = AluOpType, ActivationFunctionType
    rank = T.rank_of(core)
    nxt, prv = T.cores[(rank + 1) % N], T.cores[(rank - 1) % N]
    rid, pid, _se = topo.addr(nxt)
    mask = topo.mask(core, nxt)
    n_out, n_in = len(topo.engines(core, nxt)), len(topo.engines(prv, core))
    V, Sc, P, Y = g.vector, g.scalar, g.tensor, g.sync
    ops, sent, lead = [], [0], [0.0]
    cy = COST["cycle"]
    dur = lambda n: max(64, n) * cy
    gdur = lambda n, q: (0.05 if q == "V" else 0.065) + COST["gather"] * n * cy

    def op(forms, needs, sig=None, kind="c", nbytes=0):
        ops.append(dict(forms=forms, needs=sorted(set(x for x in needs if x is not None)), sig=sig, kind=kind, bytes=nbytes, after=[], queued=[], boost=lead[0]))
        return len(ops) - 1
    def vec(d, emit, needs):
        return op([("V", d, emit)], needs)
    def affine(on, out, a, needs, n, add=None, mul=None):
        d = lambda q: gdur(-n, q) if n < 0 else dur(n)
        if add is not None:
            fv, fs = (lambda: V.tensor_scalar(out, a, add, None, A.add)), (lambda: Sc.activation(out, a, F.Identity, bias=add))
        elif mul is not None:
            fv, fs = (lambda: V.tensor_scalar(out, a, mul, None, A.mult)), (lambda: Sc.activation(out, a, F.Identity, scale=mul))
        else:
            fv, fs = (lambda: V.tensor_copy(out, a)), (lambda: Sc.activation(out, a, F.Copy))
        return op([(q, d(q), fv if q == "V" else fs) for q in on], needs)
    def ts(out, in0, s1, s2, o0, o1, needs, n):
        if o1 is None: return vec(dur(n), lambda: V.tensor_scalar(out, in0, s1, None, o0), needs)
        return vec(dur(n), lambda: V.tensor_scalar(out, in0, s1, s2, o0, o1), needs)
    def tt(out, a, b, o, needs, n):
        return vec(gdur(-n, "V") if n < 0 else dur(n), lambda: V.tensor_tensor(out, a, b, o), needs)
    def cp(out, a, needs, n):
        return affine("V", out, a, needs, n)
    def fill(out, x, needs, n):
        return vec(dur(n), lambda: V.memset(out, x), needs)
    def mm(lst, needs, add=False, start=True, stop=True):
        def emit():
            for x, (o, l, r) in enumerate(lst):
                ins = P.matmul(o, l, r, start and (x == 0 or not add), stop and (x == len(lst) - 1 or not add))
            return ins
        return op([("P", COST["pe"] * sum(max(min(64, l.shape[-1]), r.shape[-1]) for (o, l, r) in lst), emit)], needs)
    def iota(out, pat, cm, n, base=0):
        return op([("G", 0.13 + 2 * n * cy, lambda: g.iota(out, pat, base, cm, allow_small_or_imprecise_dtypes=True))], [])
    def dma(q, pairs, sem, nbytes, needs=()):
        e = Y if q == "Y" else Sc
        def emit():
            for out, in_ in pairs[:-1]: e.dma_start(out, in_).then_inc(T.sem[sem], 16)
            return e.dma_start(*pairs[-1])
        return op([(q, 0.05 * len(pairs), emit)], list(needs), sig=(sem, 16 * len(pairs)), kind="d", nbytes=nbytes)
    def send(emit, needs, sem, cnt, n_loc, nbytes):
        sent[0] += n_loc
        a = op([("G", COST["issue"], emit)], needs, sig=("sent", None), kind="r", nbytes=nbytes)
        return op([], [a], sig=(sem, cnt), kind="a")

    qs = lambda s, a=0, b=Q: T.qall[:, s * Q + a:s * Q + b]
    ldb = [dma(e, [(T.brs[8 * x:8 * x + 8, :], T.br[:, 768 * x:768 * x + 768]) for x in (y, y + 1)], "ldb" + e, 2 * 8 * S) for e, y in (("Y", 0), ("S", 2))]
    ldq = dma("Y", [(qs(0), T.q[:])], "ldq", 256 * Q)
    lde = dma("S", [(T.ent[:], T.entry[:])], "lde", 4096)
    ldn = dma("Y", [(T.nbw[:], T.nb[:])], "ldn", 512 * S)
    ldk = dma("Y", [(T.kw[:, 0:KA], T.k[:, 0:KA])], "ldk", 256 * KA)
    ops[ldn]["after"], ops[lde]["after"], ops[ldq]["after"] = [ldq, lde], ldb, ldb
    ops[ldk]["after"] = ops[ldk]["queued"] = [ldn]

    others = [c for c in T.cores if c != core]
    def qmask(c):
        m = -1
        for d in T.cores:
            if d != c: m &= topo.mask(c, d)
        return m
    bits = lambda m: bin(m).count("1")
    def qsend(to, sem):
        ids = [DstId(rid=topo.addr(d)[0], pnc=topo.addr(d)[1]) for d in to]
        dsts = [qs((T.rank_of(d) - rank) % N) for d in to]
        tr = RemoteDMATransfer(dst_ids=ids, dma_engine_mask=qmask(core), remote_sem=T.sem[sem], srcs=[qs(0)], dsts=dsts)
        return g.remote_dma_fused([tr], local_sem=T.sem.sent)

    gp = op([("G", 0.13, lambda: g.iota(T.pi[:, 0:1], [[0, 1]], 0, 1))], [])
    ge = iota(T.ie[0:32, :], [[128, 4], [1, 144]], -16, 576, -15)
    gi = iota(T.ip[:], [[0, 8], [1, 16]], 0, 128)
    gt = iota(T.it[:], [[16, 8], [0, 2], [1, 16]], -1, 256)
    qar1 = send(lambda: qsend([nxt], "qar1"), [ldq], "qar1", bits(qmask(prv)), bits(qmask(core)), 256 * Q)
    b1 = ts(T.pb[:, 0:1], T.pi[:, 0:1], 63, None, A.bitwise_and, None, [gp], 1)
    b2 = ts(T.pb[:, 1:2], T.pi[:, 0:1], 4, None, A.arith_shift_right, None, [gp], 1)
    b3 = ts(T.pb[:, 2:3], T.pi[:, 0:1], 15, None, A.bitwise_and, None, [gp], 1)
    pf = cp(T.pf[:, 0:3], T.pb[:, 0:3], [b1, b2, b3], 3)
    row, pg, ip = T.pf[:, 0:1], T.pf[:, 1:2], T.ip[:, 0:16]
    hb = fill(T.hb[:], -float(HALF), [], 4)
    xb = ts(T.xb[:, 0:1], row, 48.0, 32768.0 + HALF, A.is_ge, A.mult, [pf], 1)
    r16 = ts(T.xb[:, 1:2], row, 16.0, None, A.is_equal, None, [pf], 1)
    rh = ts(T.xb[:, 2:3], row, 16.0, -float(HALF), A.is_equal, A.mult, [pf], 1)
    gm8 = ts(T.gm8[:], T.ip[:, 0:8], pg, None, A.is_equal, None, [pf, gi], 8)
    turn = ts(T.turn[:], T.it[:], 0.0, None, A.is_equal, None, [gt], 256)
    reset = ts(T.reset[:], T.ip[:], 0.0, -1e9, A.is_equal, A.mult, [gi], 128)
    t = [T.tmp[:, 16 * x:16 * x + 16] for x in range(9)]
    e0 = ts(t[0], ip, row, 16.0, A.is_equal, A.mult, [gi, pf], 16)
    ex = ts(t[1], ip, 32.0, row, A.add, A.is_equal, [gi, pf], 16)
    eh = ts(t[2], ip, 48.0, row, A.add, A.is_equal, [gi, pf], 16)
    u = ts(t[3], ip, -1.0, 15.0, A.mult, A.add, [gi], 16)
    ur = ts(t[4], t[3], T.xb[:, 1:2], None, A.mult, None, [u, r16], 16)
    base = tt(t[5], t[4], t[0], A.add, [ur, e0], 32)
    lo = tt(t[6], t[1], t[2], A.subtract, [ex, eh], 32)
    diag = ts(T.diag[:], ip, T.pf[:, 2:3], None, A.is_equal, None, [gi, pf], 16)
    sel = [ts(T.sel[:, 32:48], t[5], C_LO + C_HI, T.xb[:, 2:3], A.mult, A.add, [base, rh], 16),
           ts(T.sel[:, 48:64], ip, row, None, A.is_equal, None, [gi, pf], 16)]
    for x, (c, more, made) in enumerate([(C_LO, t[6], lo), (C_HI, t[2], eh)]):
        wt = ts(t[7 + x], t[5], c, None, A.mult, None, [base], 16)
        sel.append(tt(T.sel[:, 16 * x:16 * x + 16], t[7 + x], more, A.add, [wt, made], 32))
    blk = [ts(T.hb[:, 1 + c:2 + c], pg, 4.0, None, [A.is_lt, A.is_ge][c], None, [pf, hb], 1) for c in range(2)]
    sels = {m: [ts(T["sel%d" % m][:, m * c:m * c + m], T.sel[:, 0:m], T.hb[:, 1 + c:2 + c], None, A.mult, None, sel + [blk[c]], m) for c in range(2)]
            for m in (48, 64)}
    e4 = [ts(T.e4[0:32, 144 * x:144 * x + 144], T.ie[0:32, 144 * x:144 * x + 144], 0.0, None, A.is_equal, None, [ge], 144) for x in range(4)]
    PA, PT = [T["ps%d" % h] for h in range(NS)], [T["ps%d" % min(NS + x, 7)] for x in range(2)]
    ones = [fill(PA[h][:, 0:128], 1.0, [], 128) for h in range(NS)]

    brh = [affine(e, T.brh[0:32, a:a + 384], T.brs[0:32, a:a + 384], ldb + [hb], 384, add=T.hb[0:32, 0:1]) for e, a in (("V", 0), ("S", 384))]
    PB = PT[0]
    bl = [mm([(PB[:, 48 * x:48 * x + 48], T.e4[0:32, 144 * x + 15 - b:144 * x + 143 - b], T.brh[0:32, b::16]) for b in range(16)],
             brh + [e4[x]], add=True) for x in range(4)]
    blo = ts(T.blo[:], PB[:, 0:192], float(HALF), None, A.add, None, bl, 192)
    bla = send(lambda: g.remote_dma(T.bli[:], T.blo[:], T.sem.bla, T.sem.sent, pid, rid, mask), [blo, qar1 - 1], "bla", n_in, n_out, 384 * 128)
    gg = iota(T.ig[:], [[1, 8], [0, 16]], 0, 128)
    ops[gg]["after"] = [bla - 1]
    ops[qar1 - 1]["forms"] = [("G", COST["issue"] + COST["first"], ops[qar1 - 1]["forms"][0][2])]
    qarr = send(lambda: qsend([c for c in others if c != nxt], "qarr"), [ldq], "qarr", sum(bits(qmask(c)) for c in others if c != prv), bits(qmask(core)), 2 * 256 * Q)
    ops[qarr - 1]["after"] = [bla - 1]
    for i in [ge, hb, blo, bla - 1, qar1 - 1, ldq] + e4 + brh + bl + ldb: ops[i]["boost"] = 8.0
    bones = ts(T.bones[:], T.ig[:], pg, None, A.is_equal, None, [pf, gg], 128)
    z = 192 // NB2
    nb2 = [affine("VS", T.nb2[:, 16 * z * x:16 * z * (x + 1)], T.nbw[:, :].indirect(T.bli[:, z * x:z * (x + 1)]), [bla, ldn], -16 * z) for x in range(NB2)]

    qb0 = [affine("VS", T.qblk[:, x * N * Q:x * N * Q + Q], qs(0), [gm8, ldq], 64, mul=T.gm8[:, x:x + 1]) for x in range(8)]
    zero = [fill(T.qblk[:, x * N * Q + Q:(x + 1) * N * Q], 0.0, [], 192) for x in range(8)]
    qbd = dma("Y", [(T.qblk[16 * x:16 * x + 16, x * N * Q + Q:(x + 1) * N * Q], T.qall[16 * x:16 * x + 16, Q:N * Q]) for x in range(8)],
              "qbd", 3 * 256 * Q, zero + [qarr, qar1])

    ldk2 = dma("Y", [(T.kw[:, KA:S], T.k[:, KA:S])], "ldk2", 256 * (S - KA), [gg]) if KA < S else None
    ldv = dma("Y", [(T.vw[:], T.v[:])], "ldv", 256 * S, [ldn, ldk, ldk2, gg])
    def lst(k, h, a, b):
        o = 16 * k + (2 * h if k % 2 or k == 0 else COL[h])
        return T.lst[:, o + a:o + b]
    cur = [(lst(0, h, 0, w), [cp(lst(0, h, 0, w), T.ent[:, COL[h]:COL[h] + w], [lde], 8)]) for h, w in enumerate(SUBS)]
    last = [[] for _h in range(NS)]
    accin, relus = None, {PT[0].name: blo}
    for s in range(N):
        for h, W in enumerate(SUBS):
            L, rdy = cur[h]
            lead[0] = LEAD[h]
            c0, n1 = 16 * COL[h], 16 * W
            cc, cf, B = T.cu[:, c0:c0 + n1], T.ch[:, c0:c0 + n1], T.bs[0:64 * W, 128 * h:128 * h + 128]
            for step in range(2):
                far = s > 0 and step == 0
                win, have = (T.nb2 if far else T.nbw)[:, :].indirect(L), rdy + last[h] + (nb2 if far else [ldn])
                cg = cp(cc, win, have, -n1)
                c16 = affine("S", cf, win, have + [hb], -n1, add=T.hb[:, 0:1])
                tu = [mm([(PA[h][64 * c + 32:64 * c + 64, 16 * x:16 * x + 16], T.turn[:, 32 * x:32 * x + 32], T.ch[:, c0 + 16 * c:c0 + 16 * c + 16])
                          for x in range(8)], [c16, turn, ones[h]]) for c in range(W)]
                pe1, j0 = [], c0
                for cnt in PIECES[W]:
                    ga = affine("VS", T.kg[:, 16 * j0:16 * (j0 + cnt)], T.kw[:, :].indirect(T.cu[:, j0:j0 + cnt]), [cg, ldk, ldk2], -16 * cnt)
                    pe1.append(mm([(PA[h][64 * ((j - c0) // 16):64 * ((j - c0) // 16) + 16, (j % 16):128:16], T.kg[:, 16 * j:16 * j + 16],
                                    T.qblk[:, s * Q + j::N * Q]) for j in range(j0, j0 + cnt)], [ga, ones[h]] + (qb0 if s == 0 else [qbd])))
                    j0 += cnt
                ev = affine("VS", B, PA[h][0:64 * W, 0:128], pe1 + tu + [xb], 128, add=T.xb[0:64 * W, 0:1])
                k = 2 * s + step + 1
                m = 64 if k == 2 * N else 48
                K, rr = PA[h][:, 128:128 + m * W], T.rr[:, 4 * c0:4 * c0 + m * W]
                p2 = mm([(K, B, T["sel%d" % m][0:64 * W, 0:m * W])], [ev] + sels[m])
                sc = vec(dur(m * W), (lambda rr=rr, K=K, n=m * W: V.tensor_tensor_scan(rr, T.reset[:, 0:n], K, 0.0, A.add, A.max)), [p2, reset])
                top = lambda x, c: T.rr[:, 4 * c0 + m * c + 16 * x + 15:4 * c0 + m * c + 16 * x + 16]
                rdy = [ts(lst(k, h, c, c + 1), top(1, c), top(2, c), top(0, c), A.subtract, A.add, [sc], 1) for c in range(W)]
                L = lst(k, h, 0, W)
                last[h] = rdy
            if s == N - 1:
                xs = [op([("V", dur(16), lambda o=T.kq[:, s * Q + c0 + 16 * c:s * Q + c0 + 16 * c + 16], a=top(3, c): V.tensor_scalar(o, T.diag[:], a, 0.0, A.mult, A.max)),
                          ("S", dur(16), lambda o=T.kq[:, s * Q + c0 + 16 * c:s * Q + c0 + 16 * c + 16], a=top(3, c): Sc.activation(o, T.diag[:], F.Relu, scale=a))],
                         [sc, diag]) for c in range(W)]
                ps, vg = PA[h][:, 256:256 + n1], T.rs[:, s * Q + c0:s * Q + c0 + n1]
                sm = mm([(ps, T.bones[:], T.kq[:, s * Q + c0:s * Q + c0 + n1])], xs + [bones])
                val = affine("VS", vg, T.vw[:, :].indirect(L), rdy + [ldv], -n1)
                last[h] = [tt(T.term[:, s * Q + c0:s * Q + c0 + n1], vg, ps, A.mult, [sm, val], n1)]
            elif h in [x[-1] for x in SENDS]:
                hs = [x for x in SENDS if x[-1] == h][0]
                o, w = 8 * (s * NS + h), sum(SUBS[x] for x in hs)
                Li, L, sem = T.lin[:, o:o + w], lst(k, hs[0], 0, w), "la%d_%d" % (s, h)
                came = send((lambda Li=Li, L=L, sem=sem: g.remote_dma(Li, L, T.sem[sem], T.sem.sent, pid, rid, mask)), [i for x in hs for i in last[x]], sem, n_in, n_out, 1024)
                for x in hs:
                    cur[x] = (T.lin[:, o + COL[x] - COL[hs[0]]:o + COL[x] - COL[hs[0]] + SUBS[x]], [came])

        terms = []
        for x, hs in enumerate(TERMS if s < N - 1 else []):
            lead[0] = LEAD[hs[-1]]
            a, n = 16 * COL[hs[0]], 16 * sum(SUBS[h] for h in hs)
            L, rdy = lst(2 * s + 2, hs[0], 0, n // 16), [i for h in hs for i in last[h]]
            bank = PT[x % 2]
            kq, ps, rs = T.kq[:, s * Q + a:s * Q + a + n], bank[:, 0:n], T.rs[:, s * Q + a:s * Q + a + n]
            m = tt(kq, T.kw[:, :].indirect(L), qs(s, a, a + n), A.mult, rdy + [ldq, qar1, qarr, qarr][s:s + 1], -n)
            sm = mm([(ps, T.bones[:], kq)], [m, bones, relus.get(bank.name)])
            relus[bank.name] = op([("V", dur(n), lambda rs=rs, ps=ps: V.tensor_scalar(rs, ps, 0.0, None, A.max)),
                                   ("S", dur(n), lambda rs=rs, ps=ps: Sc.activation(rs, ps, F.Relu))], [sm])
            terms.append(tt(T.term[:, s * Q + a:s * Q + a + n], T.vw[:, :].indirect(L), rs, A.mult, [relus[bank.name], ldv], -n))

        def accsend(a, b, sem, s=s):
            dst, src = T.acc[:, s * Q + a:s * Q + b], T.term[:, s * Q + a:s * Q + b]
            if s == 0: return g.remote_dma(dst, src, T.sem[sem], T.sem.sent, pid, rid, mask)
            tr = RemoteDMATransfer(dst_ids=[DstId(rid=rid, pnc=pid)], dma_engine_mask=mask, remote_sem=T.sem[sem],
                                   srcs=[src, T.acc[:, (s - 1) * Q + a:(s - 1) * Q + b]], dsts=[dst], alu_op=1)
            return g.remote_dma_fused([tr], local_sem=T.sem.sent)
        if s < N - 1:
            accin = send((lambda f=accsend, s=s: f(0, Q, "aa%d" % s)), terms + [accin], "aa%d" % s, n_in, n_out, 1024 * Q)
        else:
            for x, hs in enumerate(TAILS):
                a, b = 16 * COL[hs[0]], 16 * (COL[hs[-1]] + SUBS[hs[-1]])
                fa = send((lambda f=accsend, a=a, b=b, x=x: f(a, b, "fa%d" % x)), [last[h][0] for h in hs] + [accin], "fa%d" % x, n_in, n_out, 1024 * (b - a))
                dma("Y", [(T.y[:, a:b], T.acc[:, s * Q + a:s * Q + b])], "st%d" % x, 512 * (b - a), [fa])
    return ops, sent[0]


def schedule(ops):
    wait = COST["wait"]
    lat = lambda o: {"d": COST["dma"] + o["bytes"] / COST["rate"], "r": COST["remote"] + o["bytes"] / COST["rate"]}.get(o["kind"], 0.0)
    way, users = [0.0] * len(ops), [[] for _o in ops]
    for i, o in enumerate(ops):
        for d in o["needs"] + o["after"]: users[d].append(i)
    for i in reversed(range(len(ops))):
        o = ops[i]
        way[i] = max([way[u] for u in users[i]] + [0.0]) + (min(f[1] for f in o["forms"]) + lat(o) + wait if o["forms"] else 0.0)
    way = [x + o["boost"] for x, o in zip(way, ops)]
    free, pipe, first = {q: 0.0 for q in "VSPGY"}, [0.0], [COST["first"]]
    done, began, left, order = {}, {}, [len(o["needs"] + o["after"]) for o in ops], []
    ready = [i for i, o in enumerate(ops) if not left[i]]
    while ready:
        cand = []
        for i in ready:
            at = max([done[d] for d in ops[i]["needs"]] + [began[d] for d in ops[i]["after"]] + [0.0])
            can = [(max(at, free[f[0]]), i, x, f[0], f[1]) for x, f in enumerate(ops[i]["forms"])]
            if len(can) == 2 and can[1][0] <= can[0][0] + COST["spare"]: can = can[1:]
            cand += can or [(-1.0, i, None, None, 0.0)]
        cand.sort(key=lambda c: (c[0], -way[c[1]], c[4]))
        def holds_up(c):
            for e in cand:
                if e[0] >= c[0] + c[4]: return False
                if e[3] == c[3] and way[e[1]] > way[c[1]] + COST["margin"] and c[0] + c[4] - e[0] > COST["look"] * (e[0] - c[0]):
                    if not any(z[1] == e[1] and z[3] != e[3] and z[0] <= e[0] for z in cand): return True
            return False
        t, i, x, q, d = next(c for c in cand if not holds_up(c))
        o = ops[i]
        began[i] = t
        if x is None:
            done[i] = done[o["needs"][0]]
        else:
            free[q] = t + d
            done[i] = t + d + wait
            if o["kind"] in "dr":
                half = (lat(o) - o["bytes"] / COST["rate"]) / 2
                pipe[0] = max(pipe[0], t + d + half) + o["bytes"] / COST["rate"]
                done[i] = pipe[0] + half + wait
        order.append((i, x))
        ready.remove(i)
        for u in users[i]:
            left[u] -= 1
            if left[u] == 0: ready.append(u)
    return order


def rank_program(g, core, T, topo):
    if T.rank_of(core) is None:
        return
    ops, sent = build(g, core, T, topo)
    order = schedule(ops)
    pos = {i: x for x, (i, _f) in enumerate(order)}
    queue = {"V": g.vector, "S": g.scalar, "P": g.tensor, "G": g, "Y": g.sync}
    count = {"cV": 0, "cS": 0, "cP": 0, "cG": 0}
    known = {q: {} for q in queue}
    sig, clock, stores = {}, {}, []
    for i, x in order:
        needs, sg = ops[i]["needs"], ops[i]["sig"]
        if x is None:
            sig[i], clock[i] = sg, {sg[0]: sg[1]}
            continue
        q, _d, emit = ops[i]["forms"][x]
        kn = known[q]
        for d in sorted(needs, key=lambda d: -pos[d]):
            sem, cnt = sig[d]
            if kn.get(sem, 0) >= cnt or (q == "P" and sem == "cP"): continue
            queue[q].wait_ge(T.sem[sem], cnt)
            for k2, v2 in clock[d].items():
                if kn.get(k2, 0) < v2: kn[k2] = v2
        ins = emit()
        if sg is None:
            sem = "c" + q
            count[sem] += 1
            ins.then_inc(T.sem[sem], 1)
            sig[i] = (sem, count[sem])
        elif sg[1] is None:
            sig[i] = (sg[0], 0)
        else:
            ins.then_inc(T.sem[sg[0]], 16)
            sig[i] = sg
            if sg[0].startswith("st"): stores.append(sg)
        clock[i] = dict(kn)
        clock[i][sig[i][0]] = sig[i][1]
    for sem in ("cG", "cP", "cS", "cV"):
        g.wait_ge(T.sem[sem], count[sem])
    g.wait_ge(T.sem.sent, sent)
    for sem, cnt in stores:
        g.sync.wait_ge(T.sem[sem], cnt)
